import numpy as np, ml_dtypes
CORES = [1,5,17,21,33,37,49,53]
N = 8
import mx_ref
BF = ml_dtypes.bfloat16
def gentries(a):
    return np.ascontiguousarray(a.reshape(8, 16, -1).transpose(0, 2, 1)).reshape(8, -1)
def gtable(e):
    e = np.asarray(e); return np.ascontiguousarray(e.reshape(8, -1, 16).transpose(0, 2, 1)).reshape(128, -1).astype(np.int32)
def gcols(t, e):
    v = np.concatenate([t.reshape(8, 16, -1, 4), np.zeros((8, 16, 1, 4), BF)], axis=2)
    return np.ascontiguousarray(np.stack([v[g][:, e[g]] for g in range(8)])).reshape(128, -1)
def tile(rs):
    return np.stack(rs, axis=2).reshape(128, -1).astype(BF)
def cut(t, i, w=512):
    return t[:, w * i:w * i + w]
def pick(q, e):
    c = np.concatenate([q[0].reshape(128, -1, 4), np.zeros((128, 1, 4), np.uint8)], axis=1); s = np.concatenate([q[1], np.ones((16, 1), np.uint8)], axis=1)
    return (np.ascontiguousarray(c[:, e].reshape(128, -1)), np.ascontiguousarray(s[:, e]))
def join(*qs):
    return (np.concatenate([q[0] for q in qs], axis=1), np.concatenate([q[1] for q in qs], axis=1))
def put(q, e, v):
    c, s = q[0].reshape(128, -1, 4).copy(), q[1].copy(); c[:, e] = v[0].reshape(128, -1, 4); s[:, e] = v[1]
    return (c.reshape(128, -1), s)
def pk(c, s):
    return (np.ascontiguousarray(c), mx_ref.live(s))
def emit(q):
    return q[0], q[1]
def packed(v, rng):
    q = [mx_ref.quantize(np.ascontiguousarray(v[r])) for r in range(N)]
    return np.stack([a for a, b in q]), np.stack([mx_ref.plane(b, rng) for a, b in q])
def values_of_codes():
    e, c = np.zeros((128, 128, 4), np.float32), np.zeros((128, 2, 4), np.uint8)
    e[np.arange(128), np.arange(128), 0] = 1
    c[:127, :, 0] = np.arange(256).reshape(2, 128).T[:127]
    return mx_ref.matmul(mx_ref.quantize(e.reshape(128, 512).astype(BF)), (c.reshape(128, 8), np.full((16, 2), 127, np.uint8))).T.reshape(-1).astype(np.float64)
CODE_VALUE, SCALE_VALUE = values_of_codes(), 2.0 ** (np.arange(256) - 127.0)
def decode(q):
    return (CODE_VALUE[q[0]].reshape(16, 8, -1, 4) * SCALE_VALUE[q[1]][:, None, :, None] + 0.0).reshape(128, -1).astype(np.float32)
def f(rng, *shape):
    return mx_ref.flush((rng.standard_normal(shape, dtype=np.float32) * np.exp2(rng.integers(-2, 3, shape[:-1] + (1,)))).astype(BF))
def wide(rng, *shape, cols=0):
    v = rng.standard_normal(shape, dtype=np.float32) * np.exp2(rng.integers(-12, 13, shape)).astype(np.float32)
    if cols: v *= np.repeat(np.exp2(rng.integers(-cols, cols + 1, shape[:-2] + (1, shape[-1] // 4))) * (rng.random(shape[:-2] + (1, shape[-1] // 4)) > 0.0625), 4, axis=-1).astype(np.float32)
    return mx_ref.flush(v.astype(BF))
M, P, K, L, A, R = 448, 384, 96, 192, 160, 3
def order(p):
    return np.argsort(-(p + np.float32(0.0)), axis=1, kind="stable")
def counts(e):
    return np.stack([np.bincount(e[g], minlength=M) for g in range(8)])
def gput(t, e, v):
    a, b = t.reshape(8, 16, -1, 4).copy(), v.reshape(8, 16, -1, 4)
    for g in range(8): a[g][:, e[g]] = b[g]
    return a.reshape(128, -1)
def big(v):
    v = v.astype(np.float32)
    v[np.abs(v) < np.float32(2.0 ** -16)] = 0
    return v.astype(BF)
def stored(l):
    return np.stack([gtable(e) for e in l])
def numbers_of(rng):
    return {"m": big(f(rng, N, 128, 4 * M)), "u": np.array(f(rng, N, 128, 512)), "v": np.array(f(rng, N, 128, 512)), "pt": stored(rng.integers(0, M, (N, 8, P)))}
def weights(rng, on=range(16), w=None):
    w = big(f(rng, N, 128, 2048)) if w is None else w
    w = w.reshape(N, 8, 16, 4, 8, 16, 4)
    for i in range(16):
        if i not in on:
            w[:, :, i] = 0
            w[:, :, :, :, :, i] = 0
    c, p = packed(w.reshape(N, 128, 2048), rng)
    return {"wc": c, "ws": p}
def signs(rng):
    return np.stack([rng.permutation(8) % 2 * 2.0 - 1.0 for r in range(N)])
def digits(rng, a, k, e):
    d = numbers_of(rng)
    x = d["m"].astype(np.float32).reshape(N, 8, 16, M, 4)
    s = np.arange(M) // 2
    b = ((s[:, None] >> np.arange(8)) & 1) * 2.0 ** (np.arange(8) - 23.0)
    x[:, :, 0] = 0
    x[:, :, 0, :, 0] = a[:, :, None]
    x[:, :, 8] = b[:, :4]
    x[:, :, 9] = b[:, 4:]
    x[:, :, 10:] = rng.integers(4, 8, (N, 8, 6, M, 4)) * rng.choice([-1.0, 1.0], (N, 8, 6, M, 4)) * 2.0 ** -20
    u = d["u"].reshape(N, 128, 128, 4)
    for g in range(8):
        u[:, :, 16 * g:16 * g + 2] = 0
        for j in range(2):
            u[:, 16 * g, 16 * g + j, 0] = k.astype(np.float32).astype(BF)
            u[:, 16 * g + 8:16 * g + 10, 16 * g + j] = (k * e[:, g] ** j).astype(np.float32).astype(BF)[:, None, None]
    d["m"] = x.reshape(N, 128, 4 * M).astype(BF)
    return d
def setup_inputs(rng):
    return {**numbers_of(rng), **weights(rng)}
def setup_inputs_ties(rng):
    d = numbers_of(rng)
    o = rng.permutation(N)
    x = d["m"].reshape(N, 8, 16, M, 4)
    u = d["u"].reshape(N, 8, 16, 128, 4)
    def small(*s):
        return (rng.integers(4, 8, s) * rng.choice([-1.0, 1.0], s) * 2.0 ** -30).astype(np.float32).astype(BF)
    for r in range(N):
        k = rng.permutation(M) % 3
        if o[r] == 0: k = np.zeros(M, int)
        if o[r] == 1: k = np.full(M, 2)
        a = x[r][:, :8, :3].copy()
        if o[r] % 2 == 0:
            a = small(8, 8, 3, 4)
            for j in range(2): u[r][:, :8, j::16] = small(8, 8, 8, 4)
            for g in rng.permutation(8)[:4]:
                a[g] = 0
                a[g, 0, :2, 0] = (np.array([1.0, -1.0]) * 2.0 ** -30).astype(np.float32).astype(BF)
                u[r, g, :8, 16 * g:16 * g + 2] = 0
                u[r, g, 0, 16 * g:16 * g + 2, 0] = (rng.choice([-1.0, 1.0], 2) * 2.0 ** -30).astype(np.float32).astype(BF)
        a[:, :, 2] = 0
        x[r][:, :8] = a[:, :, k]
    for g in range(8):
        e = u[:, g, :8, 16 * g:16 * g + 2].copy()
        u[:, :, :, 16 * g:16 * g + 2] = 0
        u[:, g, :8, 16 * g:16 * g + 2] = e
    return {**d, **weights(rng, range(8, 16))}
def setup_inputs_near(rng):
    l = np.sort(rng.integers(0, M, (N, 8, P)), axis=2)
    k = np.where(rng.permutation(N) < N // 2, 2.0 ** -30, 1.0)
    d = digits(rng, signs(rng), k, signs(rng))
    x = d["m"].reshape(N, 8, 16, M, 4)
    for r in range(N):
        for g in rng.permutation(8)[:4]: x[r, g, 0, l[r, g, rng.integers(P)], 0] = 2.0 ** 30
    return {**d, "pt": stored(l), **weights(rng, range(1, 8))}
def setup_inputs_shares(rng):
    o = rng.permutation(N)
    l = np.argsort(rng.random((N, 8, M)), axis=2)[:, :, :P]
    e = np.ones((N, 8))
    for r in range(N):
        if o[r] % 4 == 0: e[r] = -1
        if o[r] % 4 == 1: l[r] = l[r][:, :1].copy()
        if o[r] % 4 == 3: l[r] = l[r][:, rng.permutation(P) // 2]
    return {**digits(rng, np.ones((N, 8)), np.ones(N), e), "pt": stored(l), **weights(rng, range(1, 8))}
def setup_inputs_huge(rng):
    d = numbers_of(rng)
    o = rng.permutation(N)
    l = rng.integers(0, M, (N, 8, P))
    x = 2.0 ** 30 * (0.9 + 0.1 * rng.random((N, 8, 16, M, 4)))
    x[:, :, 15] = 2.0 ** 26 * rng.uniform(-1, 1, (N, 8, M, 4))
    for r in range(N):
        if o[r] % 2:
            c, s = rng.permutation(M) % 2, rng.permutation(P) % 2
            x[r][:, :15] *= (2.0 * c - 1.0)[:, None]
            e = np.stack([np.flatnonzero(c == i) for i in range(2)])
            l[r] = e[s[None, :], rng.integers(0, M // 2, (8, P))]
    u = d["u"].reshape(N, 128, 128, 4)
    for j in range(2):
        u[:, :, j::16] = (2.0 ** 30 * (0.9 + 0.1 * rng.random((N, 128, 8, 4))) * signs(rng)[:, None, :, None]).astype(np.float32).astype(BF)
        u[:, 15::16, j::16] = 0
    d["m"] = big(x.reshape(N, 128, 4 * M))
    return {**d, "pt": stored(l), **weights(rng, [15], rng.choice([-1.0, 1.0], (N, 128, 2048)).astype(np.float32).astype(BF))}
def setup_inputs_spread(rng):
    d = setup_inputs(rng)
    d["m"] = big(wide(rng, N, 128, 4 * M, cols=6))
    return d
def check_inputs(d):
    b = []
    for k in ("m", "u", "v"):
        a = np.abs(d[k].astype(np.float32))
        if not (np.isfinite(a).all() and ((a == 0) | (a >= 2.0 ** -30) & (a <= 2.0 ** 30)).all()): b.append("a value of " + k)
    if ((d["pt"] < 0) | (d["pt"] >= M)).any(): b.append("an entry of pt")
    if (d["wc"] % 128 == 127).any(): b.append("a code of wc that is no number")
    return b
def reference(m, u, v, pt, wc, ws):
    qu = [mx_ref.quantize(u[r]) for r in range(N)]
    lay = [pk(wc[r], ws[r]) for r in range(N)]
    pages = [m[r] for r in range(N)]
    now = [gentries(pt[r]).astype(np.int64) for r in range(N)]
    for t in range(R):
        o, wr, sent = [], [], []
        for r in range(N):
            one = gcols(pages[r], now[r])
            s = mx_ref.matmul(qu[r], mx_ref.quantize(one))
            o.append(order(s[::16]))
            wr.append(order(s[1::16])[:, :A])
            sent.append(mx_ref.quantize(gcols(one, o[r][:, :K])))
        came = decode(join(*sent)).astype(BF)
        for r in range(N):
            h = now[r].copy()
            free = np.argsort(counts(np.take_along_axis(h, o[r][:, :P - L], axis=1)) > 0, axis=1, kind="stable")
            p = gput(pages[r], free[:, :K], cut(came, (r - 1) % N, 4 * K))
            np.put_along_axis(h, o[r][:, P - L:], free[:, np.arange(L) % K], axis=1)
            at = np.take_along_axis(h, wr[r], axis=1)
            more = np.take_along_axis(counts(h), at, axis=1) > 1
            z = gcols(p, at)
            q = mx_ref.quantize(z)
            made = tile([np.maximum(mx_ref.matmul(pick(lay[r], np.arange(128 * b, 128 * b + 128)), q), np.float32(0.0)) * np.float32(0.03125) + z[:, b::4].astype(np.float32) for b in range(4)])
            i = np.argsort(np.argsort(~more, axis=1, kind="stable"), axis=1)
            to = np.where(more, np.take_along_axis(free, K + i, axis=1), at)
            np.put_along_axis(h, wr[r], to, axis=1)
            pages[r] = gput(p, to, made)
            now[r] = h
    y, om = np.zeros((N, 128, P), np.float32), np.zeros((N, 8, P), np.float32)
    oc, osc = np.zeros((N, 128, 4 * P), np.uint8), np.zeros((N, 16, P), np.uint8)
    for r in range(N):
        q = mx_ref.quantize(gcols(pages[r], now[r]))
        y[r] = mx_ref.matmul(mx_ref.quantize(v[r]), q)
        om[r] = now[r]
        oc[r], osc[r] = emit(q)
    return {"y": y, "om": om, "oc": oc, "osc": osc}

@@ -1,0 +1,584 @@
+from concourse.mybir import dt, AluOpType, ActivationFunctionType
+
+ALU = AluOpType
+ACT = ActivationFunctionType
+M, P, K, L, A, R = 448, 384, 96, 192, 160, 3
+BIG = 4.0e29
+FAR = 4096.0
+DUMP, ZQ, TWO, CP, AO, DUM = 0, 384, 768, 784, 1232, 1616
+ZS = [1632, 2176, 2720]
+END = 3264
+T0 = [[11, 12], [13, 10], [11, 12]]
+TQ = [20]
+GZ = ["VSVS", "SSSS", "SSVS"]
+GF = ["SVSV", "SSSS", "SVSV"]
+LOOK = [0.5, 1500.0, 100.0]
+NROT = 4
+
+BF, F32, I32, U16, CODE, U8 = "bfloat16", "float32", "int32", "uint16", "float8_e4m3fn_x4", "uint8"
+SCRATCH = {}
+
+
+def _sb(name, n, d):
+    SCRATCH[name] = ("sbuf", [128, n], d)
+
+
+for _n, _w, _d in [
+    ("mm", 4 * M, BF), ("ut", 512, BF), ("vt", 512, BF), ("ptl", 24, I32),
+    ("uc", 128, CODE), ("us", 128, U8), ("u2c", 256, CODE), ("u2s", 256, U8), ("vc", 128, CODE), ("vs", 128, U8),
+    ("wq", 512, CODE), ("wp", 512, U8), ("et", 2048, BF), ("ec", 512, CODE), ("es", 512, U8),
+    ("x0", 2560, BF), ("x1", 2560, BF), ("x2", 2560, BF), ("x3", 1536, BF),
+    ("qc", P, CODE), ("qs", P, U8), ("bt", 512, BF), ("zt", 640, BF), ("zc", A, CODE), ("zs", A, U8), ("rb", 640, F32),
+    ("ci", 16, I32), ("cf", 16, F32), ("ck", 64, F32), ("cu", 64, U16), ("cl", 192, F32),
+    ("c16", P, BF), ("md", P, BF), ("r0", P, BF), ("kp", P, BF), ("ones", M, BF), ("d0", M, BF),
+    ("j4", P, BF), ("sr", P, BF), ("sa", P, BF), ("nr", P, BF), ("pir", P, F32),
+    ("cz", 96, F32), ("cr", 128, F32), ("tg", 832, F32), ("page", END, F32), ("ks", 400, F32), ("kr", P, F32), ("kn", P, F32),
+    ("zer", ZS[2], BF), ("w0", ZS[0], BF), ("w1", ZS[1], BF), ("w2", ZS[2], BF),
+    ("keep", 400, BF), ("roo", 416, BF), ("roa", 416, BF), ("pf", 480, BF), ("tto", 368, BF), ("tta", 432, BF), ("ttp", 976, BF),
+    ("d1", P, F32), ("e0", P, F32), ("e1", P, F32), ("eq", P, BF), ("co0", P, BF), ("co1", P, BF),
+    ("fl0", NROT * P, BF), ("fl1", NROT * P, BF), ("sc0", 24 * 192, BF), ("sc1", 24 * 192, BF),
+    ("sg0", NROT * P, BF), ("sg1", NROT * P, BF), ("jk", NROT * P, BF), ("jq", NROT * P, BF), ("fq", 2 * P, BF), ("sq", 12 * 192, BF),
+    ("st", 320, F32), ("kq", 24, F32), ("sti", 128, I32), ("stu", 128, U16), ("kl", 48, F32), ("sb", 32, BF), ("tag", 32, F32),
+    ("se", 48, F32), ("fre", M, BF), ("mr", P, BF), ("mk", A, BF), ("pk", A, BF), ("tr", P, F32), ("yb", P, F32),
+]:
+    _sb(_n, _w, _d)
+for _r in range(R):
+    for _n, _w, _d in [("bc", 128, CODE), ("bs", 128, U8), ("lc", 128, CODE), ("ls", 128, U8), ("lu", 416, U16), ("lf", 800, F32),
+                       ("s4", 32, BF), ("rj", P, BF), ("pj", 48, BF)]:
+        _sb("%s%d" % (_n, _r), _w, _d)
+SCRATCH["pa"] = ("psum", [128, 2048], F32)
+SCRATCH["pb"] = ("psum", [128, 2048], F32)
+
+
+def v(name, lo=0, hi=None, step=1, p=None):
+    return (name, lo, SCRATCH[name][1][1] if hi is None else hi, step, p)
+
+
+def ind(win, off):
+    return ("@", win, off)
+
+
+def ap(T, x):
+    if not isinstance(x, tuple):
+        return x
+    if x[0] == "@":
+        return ap(T, x[1]).indirect(ap(T, x[2]))
+    name, lo, hi, step, p = x
+    ps = slice(0, 128) if p is None else slice(p[0], p[1], p[2])
+    return T[name][ps, lo:hi:step] if step > 1 else T[name][ps, lo:hi]
+
+
+def size(x):
+    if x[0] == "@":
+        return 16 * size(x[2])
+    return len(range(x[1], x[2], x[3]))
+
+
+def narrow(*xs):
+    return all(SCRATCH[x[0]][2] in (BF, U16) for x in xs)
+
+
+def parts(xs):
+    out = []
+    for x in xs:
+        if isinstance(x, tuple):
+            out += [x[1], x[2]] if x[0] == "@" else [x]
+    return out
+
+
+def build():
+    ops = []
+    early = [0.0]
+
+    def op(eng, fn, w, r, cost, sem=None, inc=1, lat=0.0):
+        wr, rd = [], parts(r)
+        for x in w:
+            if x[0] == "@":
+                wr.append(x[1])
+                rd.append(x[2])
+            else:
+                wr.append(x)
+        ops.append({"eng": eng, "fn": fn, "w": wr, "r": rd, "cost": cost, "sem": sem, "inc": inc, "lat": lat, "early": early[0]})
+
+    def vcost(o, i):
+        if o[0] == "@":
+            return 60 + 3.7 * size(o)
+        if i[0] == "@":
+            return 60 + 1.55 * size(o)
+        return 60 + max(30, size(o) * (0.5 if narrow(o, i) else 1.0))
+
+    def copy(o, i):
+        op("V", lambda g, T: g.vector.tensor_copy(ap(T, o), ap(T, i)), [o], [i], vcost(o, i))
+
+    def ts(o, i, s1, s2, o0, o1=None):
+        if o1 is None:
+            op("V", lambda g, T: g.vector.tensor_scalar(ap(T, o), ap(T, i), ap(T, s1), None, o0), [o], [i, s1], vcost(o, i))
+        else:
+            op("V", lambda g, T: g.vector.tensor_scalar(ap(T, o), ap(T, i), ap(T, s1), ap(T, s2), o0, o1), [o], [i, s1, s2], vcost(o, i))
+
+    def tt(o, a, b, alu):
+        two = 1.0 if (a[0] in ("pa", "pb") or b[0] in ("pa", "pb")) else 2.0
+        op("V", lambda g, T: g.vector.tensor_tensor(ap(T, o), ap(T, a), ap(T, b), alu), [o], [a, b], 60 + max(30, two * size(o)))
+
+    def scan(o, a, b, init, o0, o1):
+        op("V", lambda g, T: g.vector.tensor_tensor_scan(ap(T, o), ap(T, a), ap(T, b), init, o0, o1), [o], [a, b],
+           60 + size(o) * (0.5 if narrow(o, a, b) else 1.0))
+
+    def tr(o, i):
+        op("V", lambda g, T: g.vector.transpose(ap(T, o), ap(T, i)), [o], [i], vcost(o, i))
+
+    def mset(o, c):
+        op("V", lambda g, T: g.vector.memset(ap(T, o), c), [o], [], vcost(o, o))
+
+    def quant(c, s, i):
+        op("V", lambda g, T: g.vector.quantize_mx(ap(T, c), ap(T, s), ap(T, i)), [c, s], [i], 30 + 0.27 * size(i))
+
+    def act(o, i, f, bias=None, scale=None, acc=None):
+        def fn(g, T):
+            kw = {}
+            if bias is not None:
+                kw["bias"] = ap(T, bias)
+            if scale is not None:
+                kw["scale"] = scale
+            if acc is not None:
+                kw["accum_out"] = ap(T, acc)
+            return g.scalar.activation(ap(T, o), ap(T, i), f, **kw)
+        op("S", fn, [o] + ([acc] if acc else []), [i, bias], 78 + (1.55 if i[0] == "@" else 1.0) * size(o) + (25 if acc else 0))
+
+    def affine(o, i, scale, bias):
+        act(o, i, ACT.Identity, bias=bias, scale=scale)
+
+    def gather(eng, o, i):
+        if eng == "S":
+            act(o, i, ACT.Copy)
+        else:
+            copy(o, i)
+
+    def mx(o, wc, ws, xc, xs):
+        op("P", lambda g, T: g.tensor.matmul_mx(ap(T, o), ap(T, wc), ap(T, ws), ap(T, xc), ap(T, xs), True, True),
+           [o], [wc, ws, xc, xs], 40 + 0.7 * (size(xc) + 16))
+
+    def iota(o, pat, base, cm=0):
+        small = SCRATCH[o[0]][2] != I32
+        if small:
+            op("G", lambda g, T: g.iota(ap(T, o), pat, base, cm, allow_small_or_imprecise_dtypes=True), [o], [], 160 + 2 * size(o))
+        else:
+            op("G", lambda g, T: g.iota(ap(T, o), pat, base, cm), [o], [], 160 + 2 * size(o))
+
+    def dma(q, sem, fo, fi, w, r, lat):
+        def fn(g, T):
+            return (g.sync if q == "Y" else g.scalar).dma_start(fo(T), fi(T))
+        op(q, fn, w, r, 80, sem=sem, inc=16, lat=lat)
+
+    def mv(sem, o, i, lat=2200, q="Y"):
+        dma(q, sem, lambda T: ap(T, o), lambda T: ap(T, i), [o], [i], lat)
+
+    def u8(x):
+        return lambda T: ap(T, x).bitcast(dt.uint8)
+
+    k0, k1 = (0, 128, 16), (1, 128, 16)
+
+    early[0] = 3000.0
+    dma("Y", "ld_pl", lambda T: ap(T, v("ptl")), lambda T: T.pt[:], [v("ptl")], [], 2200)
+    early[0] = 0.0
+    dma("Y", "ld_m0", lambda T: ap(T, v("mm", 0, 896)), lambda T: T.m[:, 0:896], [v("mm", 0, 896)], [], 3500)
+    dma("S", "ld_m1", lambda T: ap(T, v("mm", 896, 1792)), lambda T: T.m[:, 896:1792], [v("mm", 896, 1792)], [], 3500)
+    dma("S", "ld_u", lambda T: ap(T, v("ut")), lambda T: T.u[:], [v("ut")], [], 2600)
+
+    def ci(i):
+        return v("ci", i, i + 1)
+
+    def cf(i):
+        return v("cf", i, i + 1)
+    iota(ci(0), [[0, 1]], 0, 1)
+    ts(ci(1), ci(0), 15, None, ALU.bitwise_and)
+    ts(ci(2), ci(0), 4, None, ALU.logical_shift_right)
+    tt(ci(3), ci(1), ci(2), ALU.add)
+    ts(ci(4), ci(3), 1, None, ALU.bitwise_and)
+    copy(cf(0), ci(1))
+    copy(cf(1), ci(4))
+    ts(cf(2), cf(0), 0.0, None, ALU.is_equal)
+    ts(cf(3), cf(0), 16.0, None, ALU.mult)
+    for i, n in ((4, K), (5, A), (6, M)):
+        ts(cf(i), cf(1), float(n + 16), cf(3), ALU.mult, ALU.add)
+    ts(cf(7), cf(0), 24.0, None, ALU.mult)
+    iota(v("ck", 14, 22), [[0, 4], [16, 2]], 0)
+    iota(v("ck", 46, 62), [[1, 2], [16, 8]], 0)
+    iota(v("cr"), [[1, 4], [0, 32]], 960)
+    iota(v("ck", 22, 46), [[1, 24]], 0)
+    iota(v("c16"), [[0, 24], [1, 16]], 0)
+    iota(v("ck", 0, 8), [[0, 8]], 0)
+    iota(v("ck", 8, 10), [[1, 2]], 1)
+    iota(v("ck", 10, 14), [[1, 2], [256, 2]], 0)
+    o_b, o_z, o_t, o_rep, o_pi, o_u = v("cu", 0, 4), v("cu", 4, 10), v("cu", 10, 14), v("cu", 14, 22), v("cu", 22, 46), v("cu", 46, 62)
+    ts(o_rep, v("ck", 14, 22), cf(0), None, ALU.add)
+    copy(o_u, v("ck", 46, 62))
+    ts(o_b, v("ck", 0, 4), cf(4), None, ALU.add)
+    ts(o_z, v("ck", 4, 10), cf(5), None, ALU.add)
+    ts(o_t, v("ck", 10, 14), cf(6), None, ALU.add)
+    ts(o_pi, v("ck", 22, 46), cf(7), None, ALU.add)
+    c_j, c_j4, c_nl, c_pf, c_p448 = v("cl", 0, 24), v("cl", 48, 72), v("cl", 72, 96), v("cl", 96, 120), v("cl", 120, 144)
+    ts(c_j, v("ck", 22, 46), 16.0, cf(0), ALU.mult, ALU.add)
+    ts(c_j4, c_j, 4.0, -960.0, ALU.mult, ALU.add)
+    iota(c_nl, [[16, 24]], 16 - 192)
+    ts(c_pf, v("ck", 22, 46), cf(7), 1.0 / 512, ALU.add, ALU.mult)
+    ts(c_p448, v("ck", 22, 46), cf(7), float(M), ALU.add, ALU.add)
+    ts(v("md"), v("c16"), cf(0), 0.5, ALU.not_equal, ALU.subtract)
+    ts(v("md"), v("md"), 2 * BIG, None, ALU.mult)
+    ts(v("r0"), v("c16"), 0.0, 0.5, ALU.is_equal, ALU.subtract)
+    ts(v("r0"), v("r0"), 2 * BIG, None, ALU.mult)
+    ts(v("kp"), v("c16"), 0.0, None, ALU.not_equal)
+    iota(v("j4"), [[4, P]], -960)
+    iota(v("cz", 0, 64), [[1, 4], [0, 16]], 960)
+    iota(v("cz", 64, 96), [[0, 32]], 192)
+    iota(v("ones"), [[0, M]], 1)
+    for lo in range(0, ZS[2], 680):
+        iota(v("zer", lo, lo + 680), [[0, 680]], 0)
+    for n in ("roo", "roa", "pf", "tto", "tta", "ttp", "keep", "rj0", "rj1", "rj2"):
+        mv("z_" + n, v(n), v("zer", AO, AO + size(v(n))))
+    iota(v("zer", TWO, TWO + 16), [[0, 16]], 2)
+    for r in range(R):
+        mv("z_w%d" % r, v("w%d" % r), v("zer", 0, ZS[r]), 3000)
+    iota(v("bt", 4 * K, 512), [[0, 128]], 0)
+    iota(v("sr"), [[1, P]], -192)
+    iota(v("sa"), [[1, 16], [16, 24]], -192)
+    mv("z_sr", v("sr", p=k1), v("sa", p=k1))
+    for b in range(4):
+        x = v("et", 512 * b, 512 * b + 512)
+        iota(x, [[0, 512]], 1)
+        op("G", lambda g, T, x=x, b=b: g.affine_select(ap(T, x), ap(T, x), [[-4, 128], [-1, 4]], ALU.is_equal, 0.0, b, 4), [x], [x], 200 + 1024)
+    quant(v("ec"), v("es"), v("et"))
+    ts(v("d0"), v("ones"), cf(2), None, ALU.mult)
+    iota(v("pir"), [[1, 24], [24, 16]], 0)
+    iota(v("ks"), [[0, 400]], 1000)
+    iota(v("tg"), [[0, 832]], DUM - AO)
+    for lo in range(0, END, 816):
+        iota(v("page", lo, lo + 816), [[1, 816]], lo - CP)
+
+    quant(v("uc"), v("us"), v("ut"))
+    op("V", lambda g, T: g.vector.tensor_copy(ap(T, v("u2c")).bitcast(dt.uint32), ap(T, v("uc")).bitcast(dt.uint32).indirect(ap(T, o_u))),
+       [v("u2c")], [v("uc"), o_u], 60 + 1.55 * 256)
+    act(v("u2s"), ind(v("us"), o_u), ACT.Copy)
+
+    def spread4(dst, tmp, src):
+        tt(tmp, ind(src, o_rep), v("cr"), ALU.add)
+        copy(dst, tmp)
+
+    t4 = v("st", 32, 56)
+    mset(v("st", 56, 64), 0.0)
+    ts(t4, v("ptl"), 4.0, -960.0, ALU.mult, ALU.add)
+    spread4(v("stu"), v("st", 64, 192), v("st", 32, 64))
+    for b in range(4):
+        gather("VS"[b % 2], v("x0", b, 4 * P, 4), ind(v("mm"), v("stu", 32 * b, 32 * b + 24)))
+    early[0] = 1.0e6
+    tt(v("kq"), v("ptl"), c_pf, ALU.add)
+    for k in range(16):
+        mv("s_r", v("kr", p=(k, 128, 16)), v("kq"), q="YS"[k % 2])
+    early[0] = 0.0
+    dma("Y", "ld_wc", u8(v("wq")), lambda T: T.wc[:], [v("wq")], [v("x0", 0, 2)], 3500)
+    dma("Y", "ld_ws", lambda T: ap(T, v("wp")), lambda T: T.ws[:], [v("wp")], [v("x0", 0, 2)], 3000)
+    dma("Y", "ld_v", lambda T: ap(T, v("vt")), lambda T: T.v[:], [v("vt")], [v("x0", 0, 2)], 3000)
+    quant(v("vc"), v("vs"), v("vt"))
+
+    def classes():
+        tq = TQ[0]
+        for t in range(24):
+            if t < tq:
+                act(v("jq", P * (t % NROT), P * (t % NROT) + P), v("kr"), ACT.Sign, bias=v("kq", t, t + 1), scale=-1.0,
+                    acc=v("st", 216 + t, 217 + t))
+            else:
+                z, y = P * (t % 2), 192 * (t - tq)
+                ts(v("fq", z, z + P), v("kr"), v("kq", t, t + 1), None, ALU.is_lt)
+                scan(v("sq", y, y + 192), v("fq", z, z + 192), v("fq", z + 192, z + P), -192.0, ALU.add, ALU.add)
+        act(v("kn"), ind(v("kr"), o_pi), ACT.Copy)
+        q_u = v("lu0", 384, 408)
+        ts(v("se", 0, tq), v("st", 216, 216 + tq), 383.0 + 2 * ZQ, 0.5, ALU.add, ALU.mult)
+        if tq < 24:
+            ts(v("se", tq, 24), v("sq", 191, 192 * (24 - tq), 192), 192.0 + ZQ, None, ALU.add)
+        ts(q_u, v("se", 0, 24), -float(ZQ), None, ALU.add)
+        ts(v("se", 24, 48), v("ptl"), float(CP), None, ALU.add)
+        copy(ind(v("ks", 0, P), q_u), v("kn"))
+        mv("s_k", v("kl", 0, 24), v("ks", 0, P, p=k0))
+        mv("s_k", v("kl", 24, 48), v("ks", 1, P + 1, p=k0))
+        ts(v("st", 240, 288), v("kl"), -0.5 + 1.0 / 1024, None, ALU.add)
+        copy(v("sti", 0, 48), v("st", 240, 288))
+        tt(v("sb", 0, 24), v("sti", 0, 24), v("sti", 24, 48), ALU.is_equal)
+        mv("s_e", v("keep", 1, P + 1, p=k0), v("sb", 0, 24))
+        mv("s_e", v("keep", 1, P + 1, p=k1), v("sb", 0, 24))
+        ts(v("sti", 48, 72), v("sti", 0, 24), 15, None, ALU.bitwise_and)
+        ts(v("sti", 72, 96), v("sti", 0, 24), 4, None, ALU.logical_shift_right)
+        ts(v("st", 240, 264), v("sti", 48, 72), 28.0, None, ALU.mult)
+        tt(v("st", 264, 288), v("st", 240, 264), v("sti", 72, 96), ALU.add)
+        tt(v("st", 288, 312), v("sb", 0, 24), c_p448, ALU.mult)
+        tt(v("st", 240, 264), v("st", 264, 288), v("st", 288, 312), ALU.max)
+        copy(q_u, v("st", 240, 264))
+        copy(ind(v("tg"), q_u), v("pir"))
+        mv("s_t", v("tag", 0, 28), v("tg", 0, M, p=k0))
+        copy(v("lu0", 384, 412), v("tag", 0, 28))
+
+    def rank(r, o, out):
+        lf = "lf%d" % r
+        bv, bs = 1024 * o, 1024 * o + 512
+        e, co, fl, sc, sg = "e%d" % o, "co%d" % o, "fl%d" % o, "sc%d" % o, "sg%d" % o
+        t0 = T0[r][o]
+        a0 = 96 * o
+        tt(v("d1"), v("pa", bv, bv + P), v("md"), ALU.max)
+        scan(v(e), v("r0"), v("d1"), 0.0, ALU.max, ALU.min)
+        tt(v("eq"), v("pa", bv, bv + P), v(e), ALU.is_equal)
+        scan(v(co), v("kp"), v("eq"), 0.0, ALU.mult, ALU.add)
+        tt(v(lf, a0 + 48, a0 + 48 + t0), v("cl", 72, 72 + t0), v(co, 15, 16 * t0, 16), ALU.subtract)
+        for t in range(24):
+            n, s = 16 * t + 16, v(e, 16 * t + 15, 16 * t + 16)
+            z = P * (t % NROT)
+            if t < t0:
+                act(v(sg, z, z + P), v("pa", bs, bs + P), ACT.Sign, bias=s, scale=-1.0)
+                act(v("jk", z, z + n), v(sg, z, z + n), ACT.Relu, acc=v(lf, a0 + t, a0 + t + 1))
+                act(v("jk", z + n, z + P), v(sg, z + n, z + P), ACT.Relu, scale=-1.0, acc=v(lf, a0 + 24 + t, a0 + 25 + t))
+            else:
+                ts(v(fl, z, z + n), v("pa", bv, bv + n), s, None, ALU.is_ge)
+                if n < P:
+                    ts(v(fl, z + n, z + P), v("pa", bv + n, bv + P), s, None, ALU.is_gt)
+                scan(v(sc, 192 * t, 192 * t + 192), v(fl, z, z + 192), v(fl, z + 192, z + P), -192.0, ALU.add, ALU.add)
+        tt(v(lf, out + t0, out + 24), v(sc, 192 * t0 + 191, 192 * 24, 192), v(co, 16 * t0 + 15, P, 16), ALU.subtract)
+        tt(v(lf, a0 + 72, a0 + 72 + t0), v(lf, a0 + 24, a0 + 24 + t0), v(lf, a0, a0 + t0), ALU.subtract)
+        tt(v(lf, out, out + t0), v(lf, a0 + 72, a0 + 72 + t0), v(lf, a0 + 48, a0 + 48 + t0), ALU.add)
+
+    def to_list(row, n, tb):
+        tr(v(tb, 0, n), v(row, 16, 16 + n))
+        tr(v(tb, n, 2 * n + 32), v(row, 0, n + 32))
+
+    for r in range(R):
+        x, xn, lu, lf, w = "x%d" % r, "x%d" % (r + 1), "lu%d" % r, "lf%d" % r, "w%d" % r
+
+        def f(i, n=24, lf=lf):
+            return v(lf, 192 + 24 * i, 192 + 24 * i + n)
+        ro, ra = f(0), f(1)
+        quant(v("qc"), v("qs"), v(x, 0, 4 * P))
+        for i in range(4):
+            c = 128 * (i // 2)
+            mx(v("pa", 512 * i, 512 * i + P), v("u2c", c, c + 128), v("u2s", c, c + 128), v("qc"), v("qs"))
+        rank(r, 0, 192)
+        ts(v(lu, 0, 24), ro, 192.0, None, ALU.add)
+        copy(ind(v("roo", 16, 400), v(lu, 0, 24)), v("j4"))
+        to_list("roo", K, "tto")
+        tt(v(lf, 672, 736), ind(v("tto"), o_b), v("cz", 0, 64), ALU.add)
+        copy(v(lu, 48, 112), v(lf, 672, 736))
+        for b in range(4):
+            gather("S", v("bt", b, 4 * K, 4), ind(v(x, 0, 4 * P), v(lu, 48 + 16 * b, 54 + 16 * b)))
+        bc, bs, lc, ls = v("bc%d" % r), v("bs%d" % r), v("lc%d" % r), v("ls%d" % r)
+        quant(bc, bs, v("bt"))
+        op("G", ("send", r, 0), [lc], [bc], 400, sem="arr%d" % r, inc=4, lat=4500)
+        op("G", ("send", r, 1), [ls], [bs], 400, sem="arr%d" % r, inc=4, lat=4500)
+        for b in range(4):
+            mx(v("pb", 512 * b, 512 * b + 128), v("ec", 128 * b, 128 * b + 128), v("es", 128 * b, 128 * b + 128), lc, ls)
+            act(v(x, 4 * P + b, 4 * (P + K), 4), v("pb", 512 * b, 512 * b + K), ACT.Copy)
+        h, u_, km, k2 = f(2), f(3), f(5), f(4)
+        s4 = v("s4%d" % r, 0, 24)
+        ts(h, ro, 96.0, -96.0, ALU.is_ge, ALU.mult)
+        ts(u_, ro, 0.0, -FAR, ALU.is_lt, ALU.mult)
+        tt(f(6), h, u_, ALU.add)
+        tt(km, ro, f(6), ALU.add)
+        ts(f(7), km, 4.0, 4.0 * P - 960.0, ALU.mult, ALU.add)
+        tt(s4, f(7), c_j4, ALU.max)
+        mv("r_s%d" % r, v("sr", p=k0), s4)
+        act(v("nr"), ind(v("sr"), o_pi), ACT.Copy)
+        rank(r, 1, 216)
+        ts(v(lu, 24, 48), ra, 192.0, None, ALU.add)
+        copy(ind(v("roa", 16, 400), v(lu, 24, 48)), v("nr"))
+        to_list("roa", A, "tta")
+        tt(v(lf, 576, 672), ind(v("tta"), o_z), v("cz"), ALU.add)
+        copy(v(lu, 112, 208), v(lf, 576, 672))
+        for b in range(4):
+            gather(GZ[r][b], v("zt", b, 4 * A, 4), ind(v(x, 0, 4 * (P + K)), v(lu, 112 + 16 * b, 122 + 16 * b)))
+        quant(v("zc"), v("zs"), v("zt"))
+        ts(f(8), ra, float(A - 192), -FAR, ALU.is_ge, ALU.mult)
+        tt(f(9), ra, f(8), ALU.add)
+        ts(f(8), f(9), 4.0, 4.0 * (P + K + 192) - 960.0, ALU.mult, ALU.add)
+        mset(v(lf, 192 + 264, 192 + 272), 0.0)
+        tt(f(10), f(8), s4, ALU.max)
+        spread4(v(lu, 208, 336), v(lf, 672, 800), f(10, 32))
+        for b in range(4):
+            mx(v("pb", 512 * b, 512 * b + A), v("wq", 128 * b, 128 * b + 128), v("wp", 128 * b, 128 * b + 128), v("zc"), v("zs"))
+            act(v("rb", A * b, A * b + A), v("pb", 512 * b, 512 * b + A), ACT.Relu, scale=0.03125)
+            tt(v(x, 4 * (P + K) + b, 2560, 4), v("rb", A * b, A * b + A), v("zt", b, 4 * A, 4), ALU.add)
+        for b in range(4):
+            gather(GF[r][b], v(xn, b, 4 * P, 4), ind(v(x), v(lu, 208 + 32 * b, 232 + 32 * b)))
+
+        if r == 0:
+            classes()
+        tt(f(13), ro, u_, ALU.subtract)
+        affine(f(14), u_, -1.0, float(TWO))
+        tt(f(13, 48), f(13, 48), v("se"), ALU.min)
+        copy(v(lu, 336, 384), f(13, 48))
+        tt(k2, km, h, ALU.add)
+        affine(f(4, 48), f(4, 48), 1.0, float(ZS[r] + K))
+        tt(v("se"), v("se"), f(4, 48), ALU.max)
+        copy(ind(v(w), v(lu, 336, 360)), v("ones", 0, P))
+        scan(v(w, AO, AO + P), v("keep", 0, P), v(w, ZQ, ZQ + P), 0.0, ALU.mult, ALU.add)
+        for s in range(r):
+            tt(v(w, ZS[s] + K, ZS[s] + 2 * K), v(w, ZS[s] + K, ZS[s] + 2 * K), v(w, ZS[s], ZS[s] + K), ALU.add)
+        act(v(w, CP, CP + M), ind(v(w, AO, ZS[r]), v(lu, 384, 412)), ACT.Copy)
+        act(v("mr"), ind(v(w), v(lu, 360, 384)), ACT.Sign, bias=-1.5)
+        act(v("mk"), ind(v("mr"), v(lu, 176, 186)), ACT.Relu)
+        scan(v("pk"), v("d0", 0, A), v("mk"), 0.0, ALU.mult, ALU.add)
+        copy(ind(v("rj%d" % r), v(lu, 192, 202)), v("pk"))
+        pj = "pj%d" % r
+        mv("r_p%d" % r, v(pj, 0, 24), v("rj%d" % r, p=k0))
+        mv("r_p%d" % r, v(pj, 24, 48), v("rj%d" % r, p=k1))
+        act(v("fre"), v(w, CP, CP + M), ACT.Relu, bias=1.0, scale=-1.0)
+        scan(v("pf", 16, 16 + M), v("d0"), v("fre"), -224.0, ALU.mult, ALU.add)
+        to_list("pf", M, "ttp")
+        pl = 512
+        act(v(lf, pl, pl + 64), ind(v("ttp"), o_t), ACT.Copy)
+        affine(v(lf, pl + 32, pl + 60), v(lf, pl + 32, pl + 60), FAR, float(223 + ZS[r] + K - AO) - FAR)
+        tt(v(lf, pl, pl + 28), v(lf, pl, pl + 28), v(lf, pl + 32, pl + 60), ALU.add)
+        tt(v("tag", 0, 28), v("tag", 0, 28), v(lf, pl, pl + 28), ALU.max)
+        nu = "lu%d" % (r + 1) if r + 1 < R else "stu"
+        n0 = 384 if r + 1 < R else 0
+        copy(v(nu, n0, n0 + 28), v("tag", 0, 28))
+        affine(f(12), v(pj, 24, 48), FAR, float(ZS[r] + 2 * K - 1) - FAR)
+        tt(f(11), f(12), v(pj, 0, 24), ALU.add)
+        if r + 1 < R:
+            tt(v("se", 0, 24), v("se", 0, 24), f(11), ALU.max)
+        tt(v("se", 24, 48), v("se", 24, 48), f(11), ALU.max)
+
+    copy(ind(v("page", AO, END), v("stu", 0, 28)), v("page", CP, CP + M))
+    copy(v("stu", 32, 56), v("se", 24, 48))
+    act(v("tr"), ind(v("page"), v("stu", 32, 56)), ACT.Copy)
+    dma("S", "o_m", lambda T: T.om[:], lambda T: ap(T, v("tr", p=k0)), [], [v("tr")], 2200)
+    quant(v("qc"), v("qs"), v("x3"))
+    mx(v("pa", 0, P), v("vc"), v("vs"), v("qc"), v("qs"))
+    dma("Y", "o_c", lambda T: T.oc[:], u8(v("qc")), [], [v("qc")], 3000)
+    for k in range(4):
+        dma("Y", "o_c", lambda T, k=k: T.osc[4 * k:4 * k + 4, :], lambda T, k=k: T.qs[32 * k:32 * k + 4, :], [], [v("qs")], 2200)
+    copy(v("yb"), v("pa", 0, P))
+    dma("Y", "o_y", lambda T: T.y[:], lambda T: ap(T, v("yb")), [], [v("yb")], 3000)
+    return ops
+
+
+def region(x):
+    name, lo, hi, step, p = x
+    if SCRATCH[name][0] == "psum":
+        lo, hi, step = lo // 512 * 512, (hi + 511) // 512 * 512, 1
+    if step == 1:
+        cm = ((1 << (hi - lo)) - 1) << lo
+    else:
+        cm = sum(1 << c for c in range(lo, hi, step))
+    pm = (1 << 128) - 1 if p is None else sum(1 << q for q in range(p[0], p[1], p[2]))
+    return name, cm, pm
+
+
+def plan():
+    ops = build()
+    n = len(ops)
+    hist = {}
+    groups = {}
+    for i, o in enumerate(ops):
+        if o["sem"]:
+            groups.setdefault(o["sem"], []).append(i)
+    for i, o in enumerate(ops):
+        dep = set()
+        acc = [(region(x), False) for x in o["r"]] + [(region(x), True) for x in o["w"]]
+        for (name, cm, pm), wr in acc:
+            psum = SCRATCH[name][0] == "psum"
+            for j, cj, pj, wj in hist.get(name, []):
+                if j != i and cj & cm and pj & pm and (wr or wj or (psum and ops[j]["eng"] != o["eng"])):
+                    dep.add(j)
+        for (name, cm, pm), wr in acc:
+            h = hist.setdefault(name, [])
+            if wr:
+                h[:] = [e for e in h if e[1] & ~cm or e[2] & ~pm]
+            h.append((i, cm, pm, wr))
+        for j in list(dep):
+            if ops[j]["sem"]:
+                dep.update(groups[ops[j]["sem"]])
+        dep.discard(i)
+        o["dep"] = sorted(dep)
+    succ = [[] for _ in range(n)]
+    for i, o in enumerate(ops):
+        for j in o["dep"]:
+            succ[j].append(i)
+    wake = LOOK[2]
+    prio = [0.0] * n
+    for i in range(n - 1, -1, -1):
+        prio[i] = ops[i]["cost"] + ops[i]["lat"] + ops[i]["early"] + max([prio[s] + wake for s in succ[i]] + [0.0])
+    left = [len(o["dep"]) for o in ops]
+    ready_at = [0.0] * n
+    ready = {e: [] for e in "VSPGY"}
+    for i in range(n):
+        if left[i] == 0:
+            ready[ops[i]["eng"]].append(i)
+    free = {e: 0.0 for e in ready}
+    order = []
+    while len(order) < n:
+        best = None
+        for e, lst in ready.items():
+            if lst:
+                t = max(free[e], min(ready_at[i] for i in lst))
+                if best is None or t < best[0]:
+                    best = (t, e)
+        t, e = best
+        top = max(ready[e], key=lambda i: prio[i])
+        now = [i for i in ready[e] if ready_at[i] <= t]
+        i = max(now, key=lambda i: prio[i])
+        if ready_at[top] > t and ready_at[top] - t < LOOK[0] * ops[i]["cost"] and prio[top] > prio[i] + LOOK[1]:
+            i, t = top, ready_at[top]
+        ready[e].remove(i)
+        ops[i]["start"] = t
+        free[e] = t + ops[i]["cost"]
+        done = free[e] + ops[i]["lat"]
+        ops[i]["done"] = done
+        order.append(i)
+        for s in succ[i]:
+            ready_at[s] = max(ready_at[s], done + wake)
+            left[s] -= 1
+            if left[s] == 0:
+                ready[ops[s]["eng"]].append(s)
+    count = {}
+    for i in order:
+        o = ops[i]
+        s = o["sem"] or "q" + o["eng"]
+        count[s] = count.get(s, 0) + o["inc"]
+        o["at"] = (s, count[s])
+    seen = {e: {} for e in ready}
+    for i in order:
+        o = ops[i]
+        need = {}
+        for j in o["dep"]:
+            s, c = ops[j]["at"]
+            need[s] = max(need.get(s, 0), c)
+        o["waits"] = []
+        for s, c in sorted(need.items()):
+            if seen[o["eng"]].get(s, 0) < c:
+                seen[o["eng"]][s] = c
+                o["waits"].append((s, c))
+    return [ops[i] for i in order], count
+
+
+PLAN, COUNT = plan()
+SEMAPHORES = sorted(COUNT) + ["snt"]
+
+
+def rank_program(g, core, T, topo):
+    rank = T.rank_of(core)
+    if rank is None:
+        return
+    nxt = T.cores[(rank + 1) % len(T.cores)]
+    rid, pid = topo.addr(nxt)[:2]
+    eng = topo.engines(core, nxt)
+    masks = [sum(1 << e for e in eng[4 * i:4 * i + 4]) for i in range(2)]
+    queue = {"V": g.vector, "S": g.scalar, "P": g.tensor, "G": g, "Y": g.sync}
+    for o in PLAN:
+        q = queue[o["eng"]]
+        for s, c in o["waits"]:
+            q.wait_ge(T.sem[s], c)
+        if isinstance(o["fn"], tuple):
+            src, dst = ap(T, o["r"][0]), ap(T, o["w"][0])
+            if o["fn"][2] == 0:
+                src, dst = src.bitcast(dt.uint8), dst.bitcast(dt.uint8)
+            g.remote_dma(dst, src, T.sem[o["sem"]], T.sem["snt"], pid, rid, masks[o["fn"][2]])
+        else:
+            o["fn"](g, T).then_inc(T.sem[o["at"][0]], o["inc"])
+    for s in sorted(COUNT):
+        g.wait_ge(T.sem[s], COUNT[s])
+    g.wait_ge(T.sem["snt"], 8 * R)

@@ -5,14 +5,20 @@ ACT = ActivationFunctionType
 M, P, K, L, A, R = 448, 384, 96, 192, 160, 3
 BIG = 4.0e29
 FAR = 4096.0
+STEP = 2.0 ** -24 * (1.0 + 2.0 ** -6)
+TINY = 2.0 ** -125
 DUMP, ZQ, TWO, CP, AO, DUM = 0, 384, 768, 784, 1232, 1616
 ZS = [1632, 2176, 2720]
 END = 3264
-T0 = [[11, 12], [13, 10], [11, 12]]
-TQ = [20]
-GZ = ["VSVS", "SSSS", "SSVS"]
-GF = ["SVSV", "SSSS", "SVSV"]
-LOOK = [0.5, 1500.0, 100.0]
+T0 = [[10, 10], [11, 13], [12, 12]]
+TQ = [22]
+GZ = ["VSVS", "VSVS", "SSSS"]
+GF = ["SVSV", "SVSV", "SSVS"]
+GB = ["VSVS", "SSSS", "SSSS"]
+GD = ["VVSV", "SSSS", "SSVS"]
+LOOK = [0.0, 0.0, 70.0]
+SEED = [67, 100.0]
+TURNS = [4]
 NROT = 4
 
 BF, F32, I32, U16, CODE, U8 = "bfloat16", "float32", "int32", "uint16", "float8_e4m3fn_x4", "uint8"
@@ -32,10 +38,11 @@ for _n, _w, _d in [
     ("ci", 16, I32), ("cf", 16, F32), ("ck", 64, F32), ("cu", 64, U16), ("cl", 192, F32),
     ("c16", P, BF), ("md", P, BF), ("r0", P, BF), ("kp", P, BF), ("ones", M, BF), ("d0", M, BF),
     ("j4", P, BF), ("sr", P, BF), ("sa", P, BF), ("nr", P, BF), ("pir", P, F32),
-    ("cz", 96, F32), ("cr", 128, F32), ("tg", 832, F32), ("page", END, F32), ("ks", 400, F32), ("kr", P, F32), ("kn", P, F32),
+    ("cz", 96, F32), ("tg", 832, F32), ("page", END, F32), ("ks", 400, F32), ("kr", P, F32), ("kn", P, F32),
     ("zer", ZS[2], BF), ("w0", ZS[0], BF), ("w1", ZS[1], BF), ("w2", ZS[2], BF),
     ("keep", 400, BF), ("roo", 416, BF), ("roa", 416, BF), ("pf", 480, BF), ("tto", 368, BF), ("tta", 432, BF), ("ttp", 976, BF),
-    ("d1", P, F32), ("e0", P, F32), ("e1", P, F32), ("eq", P, BF), ("co0", P, BF), ("co1", P, BF),
+    ("d1", P, F32), ("dl", P, F32), ("su0", 2 * P, F32), ("su1", 2 * P, F32),
+    ("e0", P, F32), ("e1", P, F32), ("eq", P, BF), ("co0", P, BF), ("co1", P, BF),
     ("fl0", NROT * P, BF), ("fl1", NROT * P, BF), ("sc0", 24 * 192, BF), ("sc1", 24 * 192, BF),
     ("sg0", NROT * P, BF), ("sg1", NROT * P, BF), ("jk", NROT * P, BF), ("jq", NROT * P, BF), ("fq", 2 * P, BF), ("sq", 12 * 192, BF),
     ("st", 320, F32), ("kq", 24, F32), ("sti", 128, I32), ("stu", 128, U16), ("kl", 48, F32), ("sb", 32, BF), ("tag", 32, F32),
@@ -127,9 +134,6 @@ def build():
     def tr(o, i):
         op("V", lambda g, T: g.vector.transpose(ap(T, o), ap(T, i)), [o], [i], vcost(o, i))
 
-    def mset(o, c):
-        op("V", lambda g, T: g.vector.memset(ap(T, o), c), [o], [], vcost(o, o))
-
     def quant(c, s, i):
         op("V", lambda g, T: g.vector.quantize_mx(ap(T, c), ap(T, s), ap(T, i)), [c, s], [i], 30 + 0.27 * size(i))
 
@@ -202,32 +206,27 @@ def build():
     for i, n in ((4, K), (5, A), (6, M)):
         ts(cf(i), cf(1), float(n + 16), cf(3), ALU.mult, ALU.add)
     ts(cf(7), cf(0), 24.0, None, ALU.mult)
-    iota(v("ck", 14, 22), [[0, 4], [16, 2]], 0)
     iota(v("ck", 46, 62), [[1, 2], [16, 8]], 0)
-    iota(v("cr"), [[1, 4], [0, 32]], 960)
     iota(v("ck", 22, 46), [[1, 24]], 0)
     iota(v("c16"), [[0, 24], [1, 16]], 0)
     iota(v("ck", 0, 8), [[0, 8]], 0)
     iota(v("ck", 8, 10), [[1, 2]], 1)
     iota(v("ck", 10, 14), [[1, 2], [256, 2]], 0)
-    o_b, o_z, o_t, o_rep, o_pi, o_u = v("cu", 0, 4), v("cu", 4, 10), v("cu", 10, 14), v("cu", 14, 22), v("cu", 22, 46), v("cu", 46, 62)
-    ts(o_rep, v("ck", 14, 22), cf(0), None, ALU.add)
+    o_b, o_z, o_t, o_pi, o_u = v("cu", 0, 4), v("cu", 4, 10), v("cu", 10, 14), v("cu", 22, 46), v("cu", 46, 62)
     copy(o_u, v("ck", 46, 62))
     ts(o_b, v("ck", 0, 4), cf(4), None, ALU.add)
     ts(o_z, v("ck", 4, 10), cf(5), None, ALU.add)
     ts(o_t, v("ck", 10, 14), cf(6), None, ALU.add)
     ts(o_pi, v("ck", 22, 46), cf(7), None, ALU.add)
-    c_j, c_j4, c_nl, c_pf, c_p448 = v("cl", 0, 24), v("cl", 48, 72), v("cl", 72, 96), v("cl", 96, 120), v("cl", 120, 144)
+    c_j, c_j4, c_pf, c_p448 = v("cl", 0, 24), v("cl", 48, 72), v("cl", 96, 120), v("cl", 120, 144)
     ts(c_j, v("ck", 22, 46), 16.0, cf(0), ALU.mult, ALU.add)
     ts(c_j4, c_j, 4.0, -960.0, ALU.mult, ALU.add)
-    iota(c_nl, [[16, 24]], 16 - 192)
     ts(c_pf, v("ck", 22, 46), cf(7), 1.0 / 512, ALU.add, ALU.mult)
     ts(c_p448, v("ck", 22, 46), cf(7), float(M), ALU.add, ALU.add)
-    ts(v("md"), v("c16"), cf(0), 0.5, ALU.not_equal, ALU.subtract)
-    ts(v("md"), v("md"), 2 * BIG, None, ALU.mult)
-    ts(v("r0"), v("c16"), 0.0, 0.5, ALU.is_equal, ALU.subtract)
-    ts(v("r0"), v("r0"), 2 * BIG, None, ALU.mult)
+    ts(v("md"), v("c16"), cf(0), None, ALU.not_equal)
+    affine(v("md"), v("md"), 2 * BIG, -BIG)
     ts(v("kp"), v("c16"), 0.0, None, ALU.not_equal)
+    affine(v("r0"), v("kp"), -2 * BIG, BIG)
     iota(v("j4"), [[4, P]], -960)
     iota(v("cz", 0, 64), [[1, 4], [0, 16]], 960)
     iota(v("cz", 64, 96), [[0, 32]], 192)
@@ -260,14 +259,8 @@ def build():
        [v("u2c")], [v("uc"), o_u], 60 + 1.55 * 256)
     act(v("u2s"), ind(v("us"), o_u), ACT.Copy)
 
-    def spread4(dst, tmp, src):
-        tt(tmp, ind(src, o_rep), v("cr"), ALU.add)
-        copy(dst, tmp)
-
-    t4 = v("st", 32, 56)
-    mset(v("st", 56, 64), 0.0)
-    ts(t4, v("ptl"), 4.0, -960.0, ALU.mult, ALU.add)
-    spread4(v("stu"), v("st", 64, 192), v("st", 32, 64))
+    for b in range(4):
+        ts(v("stu", 32 * b, 32 * b + 24), v("ptl"), 4.0, float(b), ALU.mult, ALU.add)
     for b in range(4):
         gather("VS"[b % 2], v("x0", b, 4 * P, 4), ind(v("mm"), v("stu", 32 * b, 32 * b + 24)))
     early[0] = 1.0e6
@@ -322,26 +315,26 @@ def build():
         e, co, fl, sc, sg = "e%d" % o, "co%d" % o, "fl%d" % o, "sc%d" % o, "sg%d" % o
         t0 = T0[r][o]
         a0 = 96 * o
+        su = "su%d" % o
+        act(v("dl"), v("pa", bs, bs + P), ACT.Abs, bias=TINY, scale=STEP)
+        act(v(su, 0, P), v("pa", bs, bs + P), ACT.Copy)
         tt(v("d1"), v("pa", bv, bv + P), v("md"), ALU.max)
         scan(v(e), v("r0"), v("d1"), 0.0, ALU.max, ALU.min)
+        tt(v(su, P, 2 * P), v("pa", bv, bv + P), v("dl"), ALU.add)
         tt(v("eq"), v("pa", bv, bv + P), v(e), ALU.is_equal)
         scan(v(co), v("kp"), v("eq"), 0.0, ALU.mult, ALU.add)
-        tt(v(lf, a0 + 48, a0 + 48 + t0), v("cl", 72, 72 + t0), v(co, 15, 16 * t0, 16), ALU.subtract)
+        affine(v(lf, a0 + 48, a0 + 48 + t0), v(co, 15, 16 * t0, 16), -1.0, -192.0)
         for t in range(24):
             n, s = 16 * t + 16, v(e, 16 * t + 15, 16 * t + 16)
             z = P * (t % NROT)
             if t < t0:
-                act(v(sg, z, z + P), v("pa", bs, bs + P), ACT.Sign, bias=s, scale=-1.0)
-                act(v("jk", z, z + n), v(sg, z, z + n), ACT.Relu, acc=v(lf, a0 + t, a0 + t + 1))
-                act(v("jk", z + n, z + P), v(sg, z + n, z + P), ACT.Relu, scale=-1.0, acc=v(lf, a0 + 24 + t, a0 + 25 + t))
+                act(v(sg, z, z + P), v(su, n, n + P), ACT.Sign, bias=s, scale=-1.0)
+                act(v("jk", z, z + P), v(sg, z, z + P), ACT.Relu, scale=-1.0, acc=v(lf, a0 + t, a0 + t + 1))
             else:
-                ts(v(fl, z, z + n), v("pa", bv, bv + n), s, None, ALU.is_ge)
-                if n < P:
-                    ts(v(fl, z + n, z + P), v("pa", bv + n, bv + P), s, None, ALU.is_gt)
+                ts(v(fl, z, z + P), v(su, n, n + P), s, None, ALU.is_gt)
                 scan(v(sc, 192 * t, 192 * t + 192), v(fl, z, z + 192), v(fl, z + 192, z + P), -192.0, ALU.add, ALU.add)
         tt(v(lf, out + t0, out + 24), v(sc, 192 * t0 + 191, 192 * 24, 192), v(co, 16 * t0 + 15, P, 16), ALU.subtract)
-        tt(v(lf, a0 + 72, a0 + 72 + t0), v(lf, a0 + 24, a0 + 24 + t0), v(lf, a0, a0 + t0), ALU.subtract)
-        tt(v(lf, out, out + t0), v(lf, a0 + 72, a0 + 72 + t0), v(lf, a0 + 48, a0 + 48 + t0), ALU.add)
+        tt(v(lf, out, out + t0), v(lf, a0, a0 + t0), v(lf, a0 + 48, a0 + 48 + t0), ALU.add)
 
     def to_list(row, n, tb):
         tr(v(tb, 0, n), v(row, 16, 16 + n))
@@ -364,21 +357,21 @@ def build():
         tt(v(lf, 672, 736), ind(v("tto"), o_b), v("cz", 0, 64), ALU.add)
         copy(v(lu, 48, 112), v(lf, 672, 736))
         for b in range(4):
-            gather("S", v("bt", b, 4 * K, 4), ind(v(x, 0, 4 * P), v(lu, 48 + 16 * b, 54 + 16 * b)))
+            gather(GB[r][b], v("bt", b, 4 * K, 4), ind(v(x, 0, 4 * P), v(lu, 48 + 16 * b, 54 + 16 * b)))
         bc, bs, lc, ls = v("bc%d" % r), v("bs%d" % r), v("lc%d" % r), v("ls%d" % r)
         quant(bc, bs, v("bt"))
         op("G", ("send", r, 0), [lc], [bc], 400, sem="arr%d" % r, inc=4, lat=4500)
         op("G", ("send", r, 1), [ls], [bs], 400, sem="arr%d" % r, inc=4, lat=4500)
         for b in range(4):
             mx(v("pb", 512 * b, 512 * b + 128), v("ec", 128 * b, 128 * b + 128), v("es", 128 * b, 128 * b + 128), lc, ls)
-            act(v(x, 4 * P + b, 4 * (P + K), 4), v("pb", 512 * b, 512 * b + K), ACT.Copy)
+            gather(GD[r][b], v(x, 4 * P + b, 4 * (P + K), 4), v("pb", 512 * b, 512 * b + K))
         h, u_, km, k2 = f(2), f(3), f(5), f(4)
         s4 = v("s4%d" % r, 0, 24)
         ts(h, ro, 96.0, -96.0, ALU.is_ge, ALU.mult)
         ts(u_, ro, 0.0, -FAR, ALU.is_lt, ALU.mult)
         tt(f(6), h, u_, ALU.add)
         tt(km, ro, f(6), ALU.add)
-        ts(f(7), km, 4.0, 4.0 * P - 960.0, ALU.mult, ALU.add)
+        affine(f(7), km, 4.0, 4.0 * P - 960.0)
         tt(s4, f(7), c_j4, ALU.max)
         mv("r_s%d" % r, v("sr", p=k0), s4)
         act(v("nr"), ind(v("sr"), o_pi), ACT.Copy)
@@ -394,15 +387,18 @@ def build():
         ts(f(8), ra, float(A - 192), -FAR, ALU.is_ge, ALU.mult)
         tt(f(9), ra, f(8), ALU.add)
         ts(f(8), f(9), 4.0, 4.0 * (P + K + 192) - 960.0, ALU.mult, ALU.add)
-        mset(v(lf, 192 + 264, 192 + 272), 0.0)
         tt(f(10), f(8), s4, ALU.max)
-        spread4(v(lu, 208, 336), v(lf, 672, 800), f(10, 32))
+        for b in range(4):
+            ts(v(lu, 208 + 32 * b, 232 + 32 * b), f(10), 960.0 + b, None, ALU.add)
         for b in range(4):
             mx(v("pb", 512 * b, 512 * b + A), v("wq", 128 * b, 128 * b + 128), v("wp", 128 * b, 128 * b + 128), v("zc"), v("zs"))
             act(v("rb", A * b, A * b + A), v("pb", 512 * b, 512 * b + A), ACT.Relu, scale=0.03125)
             tt(v(x, 4 * (P + K) + b, 2560, 4), v("rb", A * b, A * b + A), v("zt", b, 4 * A, 4), ALU.add)
-        for b in range(4):
-            gather(GF[r][b], v(xn, b, 4 * P, 4), ind(v(x), v(lu, 208 + 32 * b, 232 + 32 * b)))
+        nc = 1 if r + 1 < R else 3
+        for c in range(nc):
+            for b in range(4):
+                lo, n = 208 + 32 * b + 8 * c, 24 // nc
+                gather(GF[r][b], v(xn, 512 * c + b, 512 * c + 64 * n, 4), ind(v(x), v(lu, lo, lo + n)))
 
         if r == 0:
             classes()
@@ -446,13 +442,15 @@ def build():
     copy(v("stu", 32, 56), v("se", 24, 48))
     act(v("tr"), ind(v("page"), v("stu", 32, 56)), ACT.Copy)
     dma("S", "o_m", lambda T: T.om[:], lambda T: ap(T, v("tr", p=k0)), [], [v("tr")], 2200)
-    quant(v("qc"), v("qs"), v("x3"))
-    mx(v("pa", 0, P), v("vc"), v("vs"), v("qc"), v("qs"))
-    dma("Y", "o_c", lambda T: T.oc[:], u8(v("qc")), [], [v("qc")], 3000)
+    for c in range(3):
+        lo, hi = 128 * c, 128 * c + 128
+        quant(v("qc", lo, hi), v("qs", lo, hi), v("x3", 4 * lo, 4 * hi))
+        mx(v("pa", 512 * c, 512 * c + 128), v("vc"), v("vs"), v("qc", lo, hi), v("qs", lo, hi))
+        dma("Y", "o_c", lambda T, lo=lo, hi=hi: T.oc[:, 4 * lo:4 * hi], u8(v("qc", lo, hi)), [], [v("qc", lo, hi)], 2500)
+        gather("SSV"[c], v("yb", lo, hi), v("pa", 512 * c, 512 * c + 128))
+        dma("Y", "o_y", lambda T, lo=lo, hi=hi: T.y[:, lo:hi], lambda T, lo=lo, hi=hi: ap(T, v("yb", lo, hi)), [], [v("yb", lo, hi)], 2500)
     for k in range(4):
-        dma("Y", "o_c", lambda T, k=k: T.osc[4 * k:4 * k + 4, :], lambda T, k=k: T.qs[32 * k:32 * k + 4, :], [], [v("qs")], 2200)
-    copy(v("yb"), v("pa", 0, P))
-    dma("Y", "o_y", lambda T: T.y[:], lambda T: ap(T, v("yb")), [], [v("yb")], 3000)
+        dma("S", "o_s", lambda T, k=k: T.osc[4 * k:4 * k + 4, :], lambda T, k=k: T.qs[32 * k:32 * k + 4, :], [], [v("qs")], 2200)
     return ops
 
 
@@ -502,45 +500,62 @@ def plan():
     prio = [0.0] * n
     for i in range(n - 1, -1, -1):
         prio[i] = ops[i]["cost"] + ops[i]["lat"] + ops[i]["early"] + max([prio[s] + wake for s in succ[i]] + [0.0])
-    left = [len(o["dep"]) for o in ops]
-    ready_at = [0.0] * n
-    ready = {e: [] for e in "VSPGY"}
+    x = SEED[0]
     for i in range(n):
-        if left[i] == 0:
-            ready[ops[i]["eng"]].append(i)
-    free = {e: 0.0 for e in ready}
-    order = []
-    while len(order) < n:
-        best = None
-        for e, lst in ready.items():
-            if lst:
-                t = max(free[e], min(ready_at[i] for i in lst))
-                if best is None or t < best[0]:
-                    best = (t, e)
-        t, e = best
-        top = max(ready[e], key=lambda i: prio[i])
-        now = [i for i in ready[e] if ready_at[i] <= t]
-        i = max(now, key=lambda i: prio[i])
-        if ready_at[top] > t and ready_at[top] - t < LOOK[0] * ops[i]["cost"] and prio[top] > prio[i] + LOOK[1]:
-            i, t = top, ready_at[top]
-        ready[e].remove(i)
-        ops[i]["start"] = t
-        free[e] = t + ops[i]["cost"]
-        done = free[e] + ops[i]["lat"]
-        ops[i]["done"] = done
-        order.append(i)
-        for s in succ[i]:
-            ready_at[s] = max(ready_at[s], done + wake)
-            left[s] -= 1
-            if left[s] == 0:
-                ready[ops[s]["eng"]].append(s)
+        x = (x * 1103515245 + 12345) % 2147483648
+        prio[i] += SEED[1] * (x / 2147483648.0)
+
+    def schedule(prio, before, after, back):
+        left = [len(x) for x in before]
+        ready_at = [ops[i]["lat"] if back else 0.0 for i in range(n)]
+        ready = {e: [] for e in "VSPGY"}
+        for i in range(n):
+            if left[i] == 0:
+                ready[ops[i]["eng"]].append(i)
+        free = {e: 0.0 for e in ready}
+        order, start, end = [], [0.0] * n, [0.0] * n
+        while len(order) < n:
+            best = None
+            for e, lst in ready.items():
+                if lst:
+                    t = max(free[e], min(ready_at[i] for i in lst))
+                    if best is None or t < best[0]:
+                        best = (t, e)
+            t, e = best
+            top = max(ready[e], key=lambda i: prio[i])
+            i = max([i for i in ready[e] if ready_at[i] <= t], key=lambda i: prio[i])
+            if ready_at[top] > t and ready_at[top] - t < LOOK[0] * ops[i]["cost"] and prio[top] > prio[i] + LOOK[1]:
+                i, t = top, ready_at[top]
+            ready[e].remove(i)
+            start[i] = t
+            free[e] = t + ops[i]["cost"]
+            end[i] = free[e] + (0.0 if back else ops[i]["lat"])
+            order.append(i)
+            for s in after[i]:
+                ready_at[s] = max(ready_at[s], end[i] + wake + (ops[s]["lat"] if back else 0.0))
+                left[s] -= 1
+                if left[s] == 0:
+                    ready[ops[s]["eng"]].append(s)
+        return order, start, end
+
+    pred = [o["dep"] for o in ops]
+    kept = None
+    for turn in range(TURNS[0]):
+        order, start, end = schedule(prio, pred, succ, False)
+        if kept is None or max(end) < kept[0]:
+            kept = (max(end), order, start, end)
+        if turn + 1 < TURNS[0]:
+            prio = schedule(end, succ, pred, True)[2]
+    order = kept[1]
+    for i in order:
+        ops[i]["start"], ops[i]["done"] = kept[2][i], kept[3][i]
     count = {}
     for i in order:
         o = ops[i]
         s = o["sem"] or "q" + o["eng"]
         count[s] = count.get(s, 0) + o["inc"]
         o["at"] = (s, count[s])
-    seen = {e: {} for e in ready}
+    seen = {e: {} for e in "VSPGY"}
     for i in order:
         o = ops[i]
         need = {}

@@ -7,18 +7,21 @@ BIG = 4.0e29
 FAR = 4096.0
 STEP = 2.0 ** -24 * (1.0 + 2.0 ** -6)
 TINY = 2.0 ** -125
-DUMP, ZQ, TWO, CP, AO, DUM = 0, 384, 768, 784, 1232, 1616
-ZS = [1632, 2176, 2720]
-END = 3264
-T0 = [[10, 10], [11, 13], [12, 12]]
-TQ = [22]
-GZ = ["VSVS", "VSVS", "SSSS"]
-GF = ["SVSV", "SVSV", "SSVS"]
-GB = ["VSVS", "SSSS", "SSSS"]
-GD = ["VVSV", "SSSS", "SSVS"]
-LOOK = [0.0, 0.0, 70.0]
-SEED = [67, 100.0]
-TURNS = [4]
+ZQ, CP, AO, DUM = 0, 384, 832, 1216
+ZS = [1232, 1872, 2512]
+END = 3152
+ZW = 208
+TQ = [24]
+NF, LEAD, PITCH, WORDS = 12, 52, 100, 1280
+CHUNKS = [4, 4, 2, 2]
+GZ = ["SSSS", "SSSS", "SSSS"]
+GF = ["SVSS", "SVSS", "SVSS"]
+GB = ["SSSS", "SSSS", "SSSS"]
+GD = ["SSSS", "SSSS", "SSSS"]
+HS = [1, 1, 1]
+LOOK = [0.3, 300.0, 70.0]
+SEED = [1, 100.0]
+TURNS = [8]
 NROT = 4
 
 BF, F32, I32, U16, CODE, U8 = "bfloat16", "float32", "int32", "uint16", "float8_e4m3fn_x4", "uint8"
@@ -35,23 +38,24 @@ for _n, _w, _d in [
     ("wq", 512, CODE), ("wp", 512, U8), ("et", 2048, BF), ("ec", 512, CODE), ("es", 512, U8),
     ("x0", 2560, BF), ("x1", 2560, BF), ("x2", 2560, BF), ("x3", 1536, BF),
     ("qc", P, CODE), ("qs", P, U8), ("bt", 512, BF), ("zt", 640, BF), ("zc", A, CODE), ("zs", A, U8), ("rb", 640, F32),
-    ("ci", 16, I32), ("cf", 16, F32), ("ck", 64, F32), ("cu", 64, U16), ("cl", 192, F32),
-    ("c16", P, BF), ("md", P, BF), ("r0", P, BF), ("kp", P, BF), ("ones", M, BF), ("d0", M, BF),
+    ("ci", 48, I32), ("cf", 16, F32), ("ck", 96, F32), ("cu", 96, U16), ("cl", 256, F32),
+    ("c16", 576, BF), ("md", P, BF), ("r0", 576, BF), ("c4", 100, BF), ("ky", 100, BF), ("dy", 96, BF),
+    ("wt", 1536, BF), ("wu", 1024, BF), ("sumc", P, CODE), ("sums", P, U8),
+    ("ones", M, BF), ("d0", M, BF),
     ("j4", P, BF), ("sr", P, BF), ("sa", P, BF), ("nr", P, BF), ("pir", P, F32),
     ("cz", 96, F32), ("tg", 832, F32), ("page", END, F32), ("ks", 400, F32), ("kr", P, F32), ("kn", P, F32),
-    ("zer", ZS[2], BF), ("w0", ZS[0], BF), ("w1", ZS[1], BF), ("w2", ZS[2], BF),
-    ("keep", 400, BF), ("roo", 416, BF), ("roa", 416, BF), ("pf", 480, BF), ("tto", 368, BF), ("tta", 432, BF), ("ttp", 976, BF),
-    ("d1", P, F32), ("dl", P, F32), ("su0", 2 * P, F32), ("su1", 2 * P, F32),
-    ("e0", P, F32), ("e1", P, F32), ("eq", P, BF), ("co0", P, BF), ("co1", P, BF),
-    ("fl0", NROT * P, BF), ("fl1", NROT * P, BF), ("sc0", 24 * 192, BF), ("sc1", 24 * 192, BF),
-    ("sg0", NROT * P, BF), ("sg1", NROT * P, BF), ("jk", NROT * P, BF), ("jq", NROT * P, BF), ("fq", 2 * P, BF), ("sq", 12 * 192, BF),
+    ("zer", ZW, BF), ("w0", ZS[0] + L + K, BF), ("w1", ZS[1] + L + K, BF), ("w2", ZS[2] + L + K, BF),
+    ("keep", 400, BF), ("roo", 416, BF), ("roa", 416, BF), ("pf", M, BF), ("tto", 368, BF), ("tta", 432, BF), ("pp", M, BF),
+    ("dx0", 576, F32), ("dx1", 576, F32), ("dl0", L, F32), ("dl1", L, F32), ("hx0", 576, F32), ("hx1", 576, F32),
+    ("fl0", 4 * WORDS, BF), ("fl1", 4 * WORDS, BF), ("fc0", WORDS, CODE), ("fc1", WORDS, CODE), ("fs0", WORDS, U8), ("fs1", WORDS, U8),
+    ("sy", 512, F32), ("gc", 96, F32), ("jq", NROT * P, BF), ("fq", 2 * P, BF), ("sq", 12 * 192, BF),
     ("st", 320, F32), ("kq", 24, F32), ("sti", 128, I32), ("stu", 128, U16), ("kl", 48, F32), ("sb", 32, BF), ("tag", 32, F32),
     ("se", 48, F32), ("fre", M, BF), ("mr", P, BF), ("mk", A, BF), ("pk", A, BF), ("tr", P, F32), ("yb", P, F32),
 ]:
     _sb(_n, _w, _d)
 for _r in range(R):
     for _n, _w, _d in [("bc", 128, CODE), ("bs", 128, U8), ("lc", 128, CODE), ("ls", 128, U8), ("lu", 416, U16), ("lf", 800, F32),
-                       ("s4", 32, BF), ("rj", P, BF), ("pj", 48, BF)]:
+                       ("s4", 32, BF), ("rj", P, BF), ("pj", 112, BF)]:
         _sb("%s%d" % (_n, _r), _w, _d)
 SCRATCH["pa"] = ("psum", [128, 2048], F32)
 SCRATCH["pb"] = ("psum", [128, 2048], F32)
@@ -97,7 +101,7 @@ def build():
     ops = []
     early = [0.0]
 
-    def op(eng, fn, w, r, cost, sem=None, inc=1, lat=0.0):
+    def op(eng, fn, w, r, cost, sem=None, inc=1, lat=0.0, grp=None):
         wr, rd = [], parts(r)
         for x in w:
             if x[0] == "@":
@@ -105,7 +109,7 @@ def build():
                 rd.append(x[2])
             else:
                 wr.append(x)
-        ops.append({"eng": eng, "fn": fn, "w": wr, "r": rd, "cost": cost, "sem": sem, "inc": inc, "lat": lat, "early": early[0]})
+        ops.append({"eng": eng, "fn": fn, "w": wr, "r": rd, "cost": cost, "sem": sem, "inc": inc, "lat": lat, "early": early[0], "grp": grp})
 
     def vcost(o, i):
         if o[0] == "@":
@@ -130,6 +134,9 @@ def build():
     def scan(o, a, b, init, o0, o1):
         op("V", lambda g, T: g.vector.tensor_tensor_scan(ap(T, o), ap(T, a), ap(T, b), init, o0, o1), [o], [a, b],
            60 + size(o) * (0.5 if narrow(o, a, b) else 1.0))
+
+    def fill(o, c):
+        op("V", lambda g, T: g.vector.memset(ap(T, o), c), [o], [], 60 + 0.5 * size(o))
 
     def tr(o, i):
         op("V", lambda g, T: g.vector.transpose(ap(T, o), ap(T, i)), [o], [i], vcost(o, i))
@@ -158,9 +165,12 @@ def build():
         else:
             copy(o, i)
 
-    def mx(o, wc, ws, xc, xs):
-        op("P", lambda g, T: g.tensor.matmul_mx(ap(T, o), ap(T, wc), ap(T, ws), ap(T, xc), ap(T, xs), True, True),
-           [o], [wc, ws, xc, xs], 40 + 0.7 * (size(xc) + 16))
+    def mx(o, wc, ws, xc, xs, start=True, stop=True, grp=None):
+        op("P", lambda g, T: g.tensor.matmul_mx(ap(T, o), ap(T, wc), ap(T, ws), ap(T, xc), ap(T, xs), start, stop),
+           [o], [wc, ws, xc, xs], 40 + 0.7 * (size(xc) + 16), grp=grp)
+
+    def select(o, i, pat, alu, base, cm):
+        op("G", lambda g, T: g.affine_select(ap(T, o), ap(T, i), pat, alu, 0.0, base, cm), [o], [i], 200 + 2 * size(o))
 
     def iota(o, pat, base, cm=0):
         small = SCRATCH[o[0]][2] != I32
@@ -203,56 +213,80 @@ def build():
     copy(cf(1), ci(4))
     ts(cf(2), cf(0), 0.0, None, ALU.is_equal)
     ts(cf(3), cf(0), 16.0, None, ALU.mult)
-    for i, n in ((4, K), (5, A), (6, M)):
+    for i, n in ((4, K), (5, A)):
         ts(cf(i), cf(1), float(n + 16), cf(3), ALU.mult, ALU.add)
     ts(cf(7), cf(0), 24.0, None, ALU.mult)
     iota(v("ck", 46, 62), [[1, 2], [16, 8]], 0)
     iota(v("ck", 22, 46), [[1, 24]], 0)
-    iota(v("c16"), [[0, 24], [1, 16]], 0)
+    ts(ci(5), ci(1), 2, None, ALU.logical_shift_right)
+    copy(cf(8), ci(5))
+    ts(cf(9), cf(8), 1024.0, -1.0 - 3072.0, ALU.mult, ALU.add)
+    ts(cf(10), cf(9), 1.0, None, ALU.add)
+    iota(v("c16"), [[0, 36], [1, 16]], 0)
+    iota(v("c4"), [[0, 25], [1, 4]], 0)
+    ts(v("ky"), v("c4"), cf(8), None, ALU.not_equal)
+    affine(v("dy"), v("ky", 0, 96), 5120.0, -4096.0)
     iota(v("ck", 0, 8), [[0, 8]], 0)
     iota(v("ck", 8, 10), [[1, 2]], 1)
-    iota(v("ck", 10, 14), [[1, 2], [256, 2]], 0)
-    o_b, o_z, o_t, o_pi, o_u = v("cu", 0, 4), v("cu", 4, 10), v("cu", 10, 14), v("cu", 22, 46), v("cu", 46, 62)
+    iota(v("ck", 64, 92), [[16, 28]], 0)
+    o_b, o_z, o_t, o_pi, o_u = v("cu", 0, 4), v("cu", 4, 10), v("cu", 64, 92), v("cu", 22, 46), v("cu", 46, 62)
     copy(o_u, v("ck", 46, 62))
     ts(o_b, v("ck", 0, 4), cf(4), None, ALU.add)
     ts(o_z, v("ck", 4, 10), cf(5), None, ALU.add)
-    ts(o_t, v("ck", 10, 14), cf(6), None, ALU.add)
+    act(v("cl", 160, 188), v("ck", 64, 92), ACT.Identity, bias=cf(0))
+    ts(v("ci", 16, 44), v("cl", 160, 188), -13.5, 1.0 / 28, ALU.add, ALU.mult)
+    ts(v("cl", 192, 220), v("ci", 16, 44), -447.0, None, ALU.mult)
+    affine(v("cl", 160, 188), v("cl", 160, 188), 16.0, 0.0)
+    tt(v("cl", 224, 252), v("cl", 160, 188), v("cl", 192, 220), ALU.add)
+    copy(o_t, v("cl", 224, 252))
     ts(o_pi, v("ck", 22, 46), cf(7), None, ALU.add)
     c_j, c_j4, c_pf, c_p448 = v("cl", 0, 24), v("cl", 48, 72), v("cl", 96, 120), v("cl", 120, 144)
     ts(c_j, v("ck", 22, 46), 16.0, cf(0), ALU.mult, ALU.add)
     ts(c_j4, c_j, 4.0, -960.0, ALU.mult, ALU.add)
     ts(c_pf, v("ck", 22, 46), cf(7), 1.0 / 512, ALU.add, ALU.mult)
     ts(c_p448, v("ck", 22, 46), cf(7), float(M), ALU.add, ALU.add)
-    ts(v("md"), v("c16"), cf(0), None, ALU.not_equal)
-    affine(v("md"), v("md"), 2 * BIG, -BIG)
-    ts(v("kp"), v("c16"), 0.0, None, ALU.not_equal)
-    affine(v("r0"), v("kp"), -2 * BIG, BIG)
+    ts(v("c16"), v("c16"), cf(0), None, ALU.not_equal)
+    affine(v("md"), v("c16", 0, P), -2 * BIG, BIG)
+    affine(v("r0"), v("c16"), 2 * BIG, -BIG)
     iota(v("j4"), [[4, P]], -960)
     iota(v("cz", 0, 64), [[1, 4], [0, 16]], 960)
     iota(v("cz", 64, 96), [[0, 32]], 192)
     iota(v("ones"), [[0, M]], 1)
-    for lo in range(0, ZS[2], 680):
-        iota(v("zer", lo, lo + 680), [[0, 680]], 0)
-    for n in ("roo", "roa", "pf", "tto", "tta", "ttp", "keep", "rj0", "rj1", "rj2"):
-        mv("z_" + n, v(n), v("zer", AO, AO + size(v(n))))
-    iota(v("zer", TWO, TWO + 16), [[0, 16]], 2)
+    fill(v("zer"), 0.0)
+    for o in range(2):
+        gaps = [(0, LEAD)] + [(LEAD + PITCH * m - 4, LEAD + PITCH * m) for m in range(1, NF)] + [(LEAD + PITCH * NF - 4, WORDS)]
+        for lo, hi in gaps:
+            act(v("fl%d" % o, 4 * lo, 4 * hi), v("zer", 0, 4 * (hi - lo)), ACT.Copy)
+    for x in (v("roo", 0, 16), v("roa", 0, 16), v("tto", 2 * K + 32), v("tta", 2 * A + 32), v("keep"), v("rj0"), v("rj1"), v("rj2")):
+        iota(x, [[0, size(x)]], 0)
     for r in range(R):
-        mv("z_w%d" % r, v("w%d" % r), v("zer", 0, ZS[r]), 3000)
+        for lo in range(0, ZS[r] + L, 320):
+            hi = min(lo + 320, ZS[r] + L)
+            iota(v("w%d" % r, lo, hi), [[0, hi - lo]], 0)
+        iota(v("w%d" % r, ZS[r] + L, ZS[r] + L + K), [[0, K]], 2)
     iota(v("bt", 4 * K, 512), [[0, 128]], 0)
     iota(v("sr"), [[1, P]], -192)
     iota(v("sa"), [[1, 16], [16, 24]], -192)
     mv("z_sr", v("sr", p=k1), v("sa", p=k1))
+    one, eye = v("wu", 0, 512), v("wu", 512, 1024)
+    fill(one, 1.0)
+    wcol, whi, wlo = v("wt", 0, 512), v("wt", 512, 1024), v("wt", 1024, 1536)
+    select(wcol, one, [[-16, 8], [0, 64]], ALU.is_ge, 0, 1)
+    select(wcol, wcol, [[16, 8], [0, 64]], ALU.is_ge, 15, -1)
+    select(wcol, wcol, [[0, 32], [1, 4], [-1, 4]], ALU.is_equal, 0, 0)
+    select(eye, one, [[-1, 128], [0, 4]], ALU.is_equal, 0, 1)
+    select(whi, eye, [[0, 32], [-1, 4], [1, 4]], ALU.is_ge, 0, 0)
+    select(wlo, eye, [[0, 32], [1, 4], [-1, 4]], ALU.is_gt, 0, 0)
+    quant(v("sumc"), v("sums"), v("wt"))
     for b in range(4):
-        x = v("et", 512 * b, 512 * b + 512)
-        iota(x, [[0, 512]], 1)
-        op("G", lambda g, T, x=x, b=b: g.affine_select(ap(T, x), ap(T, x), [[-4, 128], [-1, 4]], ALU.is_equal, 0.0, b, 4), [x], [x], 200 + 1024)
+        select(v("et", 512 * b, 512 * b + 512), one, [[-4, 128], [-1, 4]], ALU.is_equal, b, 4)
     quant(v("ec"), v("es"), v("et"))
     ts(v("d0"), v("ones"), cf(2), None, ALU.mult)
     iota(v("pir"), [[1, 24], [24, 16]], 0)
     iota(v("ks"), [[0, 400]], 1000)
     iota(v("tg"), [[0, 832]], DUM - AO)
-    for lo in range(0, END, 816):
-        iota(v("page", lo, lo + 816), [[1, 816]], lo - CP)
+    for lo in range(0, END, 394):
+        iota(v("page", lo, lo + 394), [[1, 394]], lo - CP)
 
     quant(v("uc"), v("us"), v("ut"))
     op("V", lambda g, T: g.vector.tensor_copy(ap(T, v("u2c")).bitcast(dt.uint32), ap(T, v("uc")).bitcast(dt.uint32).indirect(ap(T, o_u))),
@@ -311,30 +345,41 @@ def build():
 
     def rank(r, o, out):
         lf = "lf%d" % r
-        bv, bs = 1024 * o, 1024 * o + 512
-        e, co, fl, sc, sg = "e%d" % o, "co%d" % o, "fl%d" % o, "sc%d" % o, "sg%d" % o
-        t0 = T0[r][o]
-        a0 = 96 * o
-        su = "su%d" % o
-        act(v("dl"), v("pa", bs, bs + P), ACT.Abs, bias=TINY, scale=STEP)
-        act(v(su, 0, P), v("pa", bs, bs + P), ACT.Copy)
-        tt(v("d1"), v("pa", bv, bv + P), v("md"), ALU.max)
-        scan(v(e), v("r0"), v("d1"), 0.0, ALU.max, ALU.min)
-        tt(v(su, P, 2 * P), v("pa", bv, bv + P), v("dl"), ALU.add)
-        tt(v("eq"), v("pa", bv, bv + P), v(e), ALU.is_equal)
-        scan(v(co), v("kp"), v("eq"), 0.0, ALU.mult, ALU.add)
-        affine(v(lf, a0 + 48, a0 + 48 + t0), v(co, 15, 16 * t0, 16), -1.0, -192.0)
-        for t in range(24):
-            n, s = 16 * t + 16, v(e, 16 * t + 15, 16 * t + 16)
-            z = P * (t % NROT)
-            if t < t0:
-                act(v(sg, z, z + P), v(su, n, n + P), ACT.Sign, bias=s, scale=-1.0)
-                act(v("jk", z, z + P), v(sg, z, z + P), ACT.Relu, scale=-1.0, acc=v(lf, a0 + t, a0 + t + 1))
-            else:
-                ts(v(fl, z, z + P), v(su, n, n + P), s, None, ALU.is_gt)
-                scan(v(sc, 192 * t, 192 * t + 192), v(fl, z, z + 192), v(fl, z + 192, z + P), -192.0, ALU.add, ALU.add)
-        tt(v(lf, out + t0, out + 24), v(sc, 192 * t0 + 191, 192 * 24, 192), v(co, 16 * t0 + 15, P, 16), ALU.subtract)
-        tt(v(lf, out, out + t0), v(lf, a0, a0 + t0), v(lf, a0 + 48, a0 + 48 + t0), ALU.add)
+        dx, dl, hx, fl, fc, fs = ["%s%d" % (n, o) for n in ("dx", "dl", "hx", "fl", "fc", "fs")]
+        row, g0 = v("pa", 512 * o, 512 * o + P), 48 * o
+        tt(v(dx, L, L + P), row, v("md"), ALU.min)
+        act(v(dl), v(dx, P, L + P), ACT.Abs, bias=-TINY, scale=STEP)
+        tt(v(dx, 0, L), v("pa", 512 * o + L, 512 * o + P), v(dl), ALU.subtract)
+        scan(v(hx), v("r0"), v(dx), 0.0, ALU.min, ALU.max)
+        tt(v("gc", g0 + 24, g0 + 36), v(hx, P + 15, L + P, 16), v(hx, L + 15, P, 16), ALU.is_gt)
+        act(v("gc", g0, g0 + 12), v("gc", g0 + 24, g0 + 36), ACT.Identity, bias=cf(9))
+        act(v("gc", g0 + 12, g0 + 24), v("gc", g0 + 24, g0 + 36), ACT.Identity, bias=cf(10), scale=-1.0)
+
+        def at(m):
+            return LEAD + PITCH * (NF - 1 - m)
+        views = [(at(m), 0) for m in range(NF)] + [(at(m) + 4 * m, k) for m in range(NF + 1) for k in (1, 2)]
+        views.sort()
+        kinds = [[e for e in views if e[1] == k] for k in range(3)]
+        bank = [("pb", 0) if o == 0 else ("pa", 0), ("pa", 1024), ("pa", 1536)]
+        m, done = NF, LEAD
+        for n in CHUNKS:
+            for m in range(m - 1, m - 1 - n, -1):
+                tt(v(fl, 4 * at(m), 4 * at(m) + P), row, v(hx, L - 16 * m, L + P - 16 * m), ALU.is_gt)
+            lo, hi = done, done + PITCH * n
+            if r == 0:
+                lo, hi = (0 if lo == LEAD else lo), (WORDS if m == 0 else hi)
+            quant(v(fc, lo, hi), v(fs, lo, hi), v(fl, 4 * lo, 4 * hi))
+            done += PITCH * n
+            while views and (m == 0 or views[0][0] + 128 <= done):
+                a, k = e = views.pop(0)
+                mx(v(bank[k][0], bank[k][1], bank[k][1] + 128), v("sumc", 128 * k, 128 * k + 128), v("sums", 128 * k, 128 * k + 128),
+                   v(fc, a, a + 128), v(fs, a, a + 128), e == kinds[k][0], e == kinds[k][-1], (r, o, k))
+        act(v("sy", 0, 100), v("pa", 1024, 1124), ACT.Copy)
+        tt(v("sy", 104, 204), v("sy", 0, 100), v("pa", 1537, 1637), ALU.add)
+        scan(v("sy", 208, 308), v("ky"), v("sy", 104, 204), 0.0, ALU.mult, ALU.add)
+        tt(v("sy", 312, 408), v("sy", 211, 307), v(bank[0][0], bank[0][1], bank[0][1] + 96), ALU.subtract)
+        scan(v("sy", 416, 512), v("dy"), v("sy", 312, 408), 0.0, ALU.add, ALU.max)
+        tt(v(lf, out, out + 24), v("sy", 419, 512, 4), v("gc", g0, g0 + 24), ALU.add)
 
     def to_list(row, n, tb):
         tr(v(tb, 0, n), v(row, 16, 16 + n))
@@ -347,8 +392,8 @@ def build():
             return v(lf, 192 + 24 * i, 192 + 24 * i + n)
         ro, ra = f(0), f(1)
         quant(v("qc"), v("qs"), v(x, 0, 4 * P))
-        for i in range(4):
-            c = 128 * (i // 2)
+        for i in range(2):
+            c = 128 * i
             mx(v("pa", 512 * i, 512 * i + P), v("u2c", c, c + 128), v("u2s", c, c + 128), v("qc"), v("qs"))
         rank(r, 0, 192)
         ts(v(lu, 0, 24), ro, 192.0, None, ALU.add)
@@ -367,10 +412,11 @@ def build():
             gather(GD[r][b], v(x, 4 * P + b, 4 * (P + K), 4), v("pb", 512 * b, 512 * b + K))
         h, u_, km, k2 = f(2), f(3), f(5), f(4)
         s4 = v("s4%d" % r, 0, 24)
-        ts(h, ro, 96.0, -96.0, ALU.is_ge, ALU.mult)
-        ts(u_, ro, 0.0, -FAR, ALU.is_lt, ALU.mult)
-        tt(f(6), h, u_, ALU.add)
-        tt(km, ro, f(6), ALU.add)
+        act(f(6), ro, ACT.Sign, bias=-95.5)
+        affine(h, f(6), -48.0, -48.0)
+        act(u_, ro, ACT.Relu, bias=-FAR, scale=-2 * FAR)
+        tt(k2, ro, u_, ALU.subtract)
+        tt(km, k2, h, ALU.add)
         affine(f(7), km, 4.0, 4.0 * P - 960.0)
         tt(s4, f(7), c_j4, ALU.max)
         mv("r_s%d" % r, v("sr", p=k0), s4)
@@ -384,16 +430,19 @@ def build():
         for b in range(4):
             gather(GZ[r][b], v("zt", b, 4 * A, 4), ind(v(x, 0, 4 * (P + K)), v(lu, 112 + 16 * b, 122 + 16 * b)))
         quant(v("zc"), v("zs"), v("zt"))
-        ts(f(8), ra, float(A - 192), -FAR, ALU.is_ge, ALU.mult)
-        tt(f(9), ra, f(8), ALU.add)
-        ts(f(8), f(9), 4.0, 4.0 * (P + K + 192) - 960.0, ALU.mult, ALU.add)
-        tt(f(10), f(8), s4, ALU.max)
+        act(f(8), ra, ACT.Relu, bias=2 * FAR * (192.5 - A), scale=2 * FAR)
+        affine(f(15), ra, 4.0, 4.0 * (P + K + 192) - 960.0)
+        tt(f(9), f(15), f(8), ALU.subtract)
+        tt(f(10), f(9), s4, ALU.max)
         for b in range(4):
             ts(v(lu, 208 + 32 * b, 232 + 32 * b), f(10), 960.0 + b, None, ALU.add)
         for b in range(4):
             mx(v("pb", 512 * b, 512 * b + A), v("wq", 128 * b, 128 * b + 128), v("wp", 128 * b, 128 * b + 128), v("zc"), v("zs"))
-            act(v("rb", A * b, A * b + A), v("pb", 512 * b, 512 * b + A), ACT.Relu, scale=0.03125)
-            tt(v(x, 4 * (P + K) + b, 2560, 4), v("rb", A * b, A * b + A), v("zt", b, 4 * A, 4), ALU.add)
+            act(v("rb", b, 4 * A, 4), v("pb", 512 * b, 512 * b + A), ACT.Relu, scale=0.03125)
+            if b % HS[r] == HS[r] - 1:
+                for e in range(b + 1 - HS[r], b + 1) if HS[r] < 4 else [0]:
+                    st = 4 if HS[r] < 4 else 1
+                    tt(v(x, 4 * (P + K) + e, 2560, st), v("rb", e, 4 * A, st), v("zt", e, 4 * A, st), ALU.add)
         nc = 1 if r + 1 < R else 3
         for c in range(nc):
             for b in range(4):
@@ -402,17 +451,14 @@ def build():
 
         if r == 0:
             classes()
-        tt(f(13), ro, u_, ALU.subtract)
-        affine(f(14), u_, -1.0, float(TWO))
-        tt(f(13, 48), f(13, 48), v("se"), ALU.min)
-        copy(v(lu, 336, 384), f(13, 48))
-        tt(k2, km, h, ALU.add)
-        affine(f(4, 48), f(4, 48), 1.0, float(ZS[r] + K))
-        tt(v("se"), v("se"), f(4, 48), ALU.max)
+        affine(f(13), k2, 1.0, float(ZS[r]))
+        affine(f(14), km, 1.0, float(ZS[r] + L))
+        tt(v("se"), v("se"), f(13, 48), ALU.max)
+        copy(v(lu, 336, 384), v("se"))
         copy(ind(v(w), v(lu, 336, 360)), v("ones", 0, P))
         scan(v(w, AO, AO + P), v("keep", 0, P), v(w, ZQ, ZQ + P), 0.0, ALU.mult, ALU.add)
         for s in range(r):
-            tt(v(w, ZS[s] + K, ZS[s] + 2 * K), v(w, ZS[s] + K, ZS[s] + 2 * K), v(w, ZS[s], ZS[s] + K), ALU.add)
+            tt(v(w, ZS[s] + L, ZS[s] + L + K), v(w, ZS[s] + K, ZS[s] + L), v(w, ZS[s], ZS[s] + K), ALU.add)
         act(v(w, CP, CP + M), ind(v(w, AO, ZS[r]), v(lu, 384, 412)), ACT.Copy)
         act(v("mr"), ind(v(w), v(lu, 360, 384)), ACT.Sign, bias=-1.5)
         act(v("mk"), ind(v("mr"), v(lu, 176, 186)), ACT.Relu)
@@ -422,17 +468,18 @@ def build():
         mv("r_p%d" % r, v(pj, 0, 24), v("rj%d" % r, p=k0))
         mv("r_p%d" % r, v(pj, 24, 48), v("rj%d" % r, p=k1))
         act(v("fre"), v(w, CP, CP + M), ACT.Relu, bias=1.0, scale=-1.0)
-        scan(v("pf", 16, 16 + M), v("d0"), v("fre"), -224.0, ALU.mult, ALU.add)
-        to_list("pf", M, "ttp")
-        pl = 512
-        act(v(lf, pl, pl + 64), ind(v("ttp"), o_t), ACT.Copy)
-        affine(v(lf, pl + 32, pl + 60), v(lf, pl + 32, pl + 60), FAR, float(223 + ZS[r] + K - AO) - FAR)
-        tt(v(lf, pl, pl + 28), v(lf, pl, pl + 28), v(lf, pl + 32, pl + 60), ALU.add)
+        scan(v("pf"), v("d0"), v("fre"), -224.0, ALU.mult, ALU.add)
+        act(v("pp"), ind(v("pf"), o_t), ACT.Copy)
+        mv("r_f%d" % r, v(pj, 48, 76), v("pp", p=k0))
+        mv("r_f%d" % r, v(pj, 80, 108), v("pp", p=k1))
+        pl = 768
+        affine(v(lf, 736, 764), v(pj, 80, 108), FAR, float(223 + ZS[r] + L - AO) - FAR)
+        tt(v(lf, pl, pl + 28), v(pj, 48, 76), v(lf, 736, 764), ALU.add)
         tt(v("tag", 0, 28), v("tag", 0, 28), v(lf, pl, pl + 28), ALU.max)
         nu = "lu%d" % (r + 1) if r + 1 < R else "stu"
         n0 = 384 if r + 1 < R else 0
         copy(v(nu, n0, n0 + 28), v("tag", 0, 28))
-        affine(f(12), v(pj, 24, 48), FAR, float(ZS[r] + 2 * K - 1) - FAR)
+        affine(f(12), v(pj, 24, 48), FAR, float(ZS[r] + L + K - 1) - FAR)
         tt(f(11), f(12), v(pj, 0, 24), ALU.add)
         if r + 1 < R:
             tt(v("se", 0, 24), v("se", 0, 24), f(11), ALU.max)
@@ -532,7 +579,8 @@ def plan():
             end[i] = free[e] + (0.0 if back else ops[i]["lat"])
             order.append(i)
             for s in after[i]:
-                ready_at[s] = max(ready_at[s], end[i] + wake + (ops[s]["lat"] if back else 0.0))
+                gap = 0.0 if ops[i]["grp"] and ops[i]["grp"] == ops[s]["grp"] else wake
+                ready_at[s] = max(ready_at[s], end[i] + gap + (ops[s]["lat"] if back else 0.0))
                 left[s] -= 1
                 if left[s] == 0:
                     ready[ops[s]["eng"]].append(s)
@@ -560,6 +608,8 @@ def plan():
         o = ops[i]
         need = {}
         for j in o["dep"]:
+            if o["grp"] and o["grp"] == ops[j]["grp"]:
+                continue
             s, c = ops[j]["at"]
             need[s] = max(need.get(s, 0), c)
         o["waits"] = []

@@ -11,17 +11,20 @@ ZQ, CP, AO, DUM = 0, 384, 832, 1216
 ZS = [1232, 1872, 2512]
 END = 3152
 ZW = 208
-TQ = [24]
-NF, LEAD, PITCH, WORDS = 12, 52, 100, 1280
-CHUNKS = [4, 4, 2, 2]
-GZ = ["SSSS", "SSSS", "SSSS"]
+NF, LEAD, PITCH, WORDS = 12, 52, 100, 1284
+CHUNKS = [3, 3, 2, 2, 2]
+GZ = ["SVSV", "SVSV", "SVSV"]
 GF = ["SVSS", "SVSS", "SVSS"]
-GB = ["SSSS", "SSSS", "SSSS"]
 GD = ["SSSS", "SSSS", "SSSS"]
 HS = [1, 1, 1]
-LOOK = [0.3, 300.0, 70.0]
-SEED = [1, 100.0]
-TURNS = [8]
+LOOK = [0.3, 1000.0]
+SEED = [2, 1500.0]
+TURNS = [24]
+SEND, MOVE = 5000.0, 2500.0
+CASES = [(55.0, 20.0, 90.0, 3.1, 1.5, 0.6, 1.15, 800.0), (45.0, 20.0, 70.0, 2.5, 1.8, 0.5, 1.3, 1200.0),
+         (60.0, 20.0, 120.0, 4.5, 1.2, 0.8, 1.0, 600.0), (60.0, 30.0, 70.0, 3.7, 1.55, 0.7, 1.0, 400.0),
+         (55.0, 20.0, 90.0, 3.1, 1.6, 0.8, 1.6, 1400.0), (55.0, 20.0, 110.0, 3.1, 1.7, 0.9, 1.4, 1000.0)]
+WEIGHED = 4
 NROT = 4
 
 BF, F32, I32, U16, CODE, U8 = "bfloat16", "float32", "int32", "uint16", "float8_e4m3fn_x4", "uint8"
@@ -37,10 +40,10 @@ for _n, _w, _d in [
     ("uc", 128, CODE), ("us", 128, U8), ("u2c", 256, CODE), ("u2s", 256, U8), ("vc", 128, CODE), ("vs", 128, U8),
     ("wq", 512, CODE), ("wp", 512, U8), ("et", 2048, BF), ("ec", 512, CODE), ("es", 512, U8),
     ("x0", 2560, BF), ("x1", 2560, BF), ("x2", 2560, BF), ("x3", 1536, BF),
-    ("qc", P, CODE), ("qs", P, U8), ("bt", 512, BF), ("zt", 640, BF), ("zc", A, CODE), ("zs", A, U8), ("rb", 640, F32),
-    ("ci", 48, I32), ("cf", 16, F32), ("ck", 96, F32), ("cu", 96, U16), ("cl", 256, F32),
-    ("c16", 576, BF), ("md", P, BF), ("r0", 576, BF), ("c4", 100, BF), ("ky", 100, BF), ("dy", 96, BF),
-    ("wt", 1536, BF), ("wu", 1024, BF), ("sumc", P, CODE), ("sums", P, U8),
+    ("qc", P, CODE), ("qs", P, U8), ("df", 4 * P, BF), ("ll", 48, U16), ("zt", 640, BF), ("zc", A, CODE), ("zs", A, U8), ("rb", 640, F32),
+    ("ci", 80, I32), ("cf", 16, F32), ("ck", 96, F32), ("cu", 128, U16), ("cl", 336, F32),
+    ("c16", 576, BF), ("md", P, BF), ("r0", 576, BF), ("c4", 104, BF), ("dy", 96, BF),
+    ("wt", 2048, BF), ("wu", 512, BF), ("sumc", 512, CODE), ("sums", 512, U8),
     ("ones", M, BF), ("d0", M, BF),
     ("j4", P, BF), ("sr", P, BF), ("sa", P, BF), ("nr", P, BF), ("pir", P, F32),
     ("cz", 96, F32), ("tg", 832, F32), ("page", END, F32), ("ks", 400, F32), ("kr", P, F32), ("kn", P, F32),
@@ -48,14 +51,14 @@ for _n, _w, _d in [
     ("keep", 400, BF), ("roo", 416, BF), ("roa", 416, BF), ("pf", M, BF), ("tto", 368, BF), ("tta", 432, BF), ("pp", M, BF),
     ("dx0", 576, F32), ("dx1", 576, F32), ("dl0", L, F32), ("dl1", L, F32), ("hx0", 576, F32), ("hx1", 576, F32),
     ("fl0", 4 * WORDS, BF), ("fl1", 4 * WORDS, BF), ("fc0", WORDS, CODE), ("fc1", WORDS, CODE), ("fs0", WORDS, U8), ("fs1", WORDS, U8),
-    ("sy", 512, F32), ("gc", 96, F32), ("jq", NROT * P, BF), ("fq", 2 * P, BF), ("sq", 12 * 192, BF),
-    ("st", 320, F32), ("kq", 24, F32), ("sti", 128, I32), ("stu", 128, U16), ("kl", 48, F32), ("sb", 32, BF), ("tag", 32, F32),
-    ("se", 48, F32), ("fre", M, BF), ("mr", P, BF), ("mk", A, BF), ("pk", A, BF), ("tr", P, F32), ("yb", P, F32),
+    ("sy", 512, F32), ("gc", 96, F32), ("jq", NROT * P, BF), ("cod", END, BF), ("cr", 2 * P, BF), ("lv", 128, U16), ("pz", 2 * A + 16, BF),
+    ("st", 320, F32), ("kq", 24, F32), ("sti", 128, I32), ("stu", 128, U16), ("kl", 48, F32), ("sb", 32, F32), ("tag", 32, F32),
+    ("se", 48, F32), ("fre", M, BF), ("mr", P, BF), ("mk", A, BF), ("pk", P, BF), ("pn", P, BF), ("tr", P, F32), ("yb", P, F32),
 ]:
     _sb(_n, _w, _d)
 for _r in range(R):
-    for _n, _w, _d in [("bc", 128, CODE), ("bs", 128, U8), ("lc", 128, CODE), ("ls", 128, U8), ("lu", 416, U16), ("lf", 800, F32),
-                       ("s4", 32, BF), ("rj", P, BF), ("pj", 112, BF)]:
+    for _n, _w, _d in [("bc", P, CODE), ("bs", P, U8), ("lc", P, CODE), ("ls", P, U8), ("lu", 416, U16), ("lf", 800, F32),
+                       ("s4", 32, BF), ("rj", P, BF), ("pj", 136, BF)]:
         _sb("%s%d" % (_n, _r), _w, _d)
 SCRATCH["pa"] = ("psum", [128, 2048], F32)
 SCRATCH["pb"] = ("psum", [128, 2048], F32)
@@ -99,7 +102,7 @@ def parts(xs):
 
 def build():
     ops = []
-    early = [0.0]
+    early, late = [0.0], [False]
 
     def op(eng, fn, w, r, cost, sem=None, inc=1, lat=0.0, grp=None):
         wr, rd = [], parts(r)
@@ -109,14 +112,15 @@ def build():
                 rd.append(x[2])
             else:
                 wr.append(x)
-        ops.append({"eng": eng, "fn": fn, "w": wr, "r": rd, "cost": cost, "sem": sem, "inc": inc, "lat": lat, "early": early[0], "grp": grp})
+        ops.append({"eng": eng, "fn": fn, "w": wr, "r": rd, "cost": cost, "sem": sem, "inc": inc, "lat": lat, "early": early[0], "grp": grp,
+                    "late": late[0] and eng == "G"})
 
     def vcost(o, i):
         if o[0] == "@":
-            return 60 + 3.7 * size(o)
+            return ("scatter", size(o))
         if i[0] == "@":
-            return 60 + 1.55 * size(o)
-        return 60 + max(30, size(o) * (0.5 if narrow(o, i) else 1.0))
+            return ("gather", size(o))
+        return ("plain", size(o) * (0.5 if narrow(o, i) else 1.0))
 
     def copy(o, i):
         op("V", lambda g, T: g.vector.tensor_copy(ap(T, o), ap(T, i)), [o], [i], vcost(o, i))
@@ -129,20 +133,20 @@ def build():
 
     def tt(o, a, b, alu):
         two = 1.0 if (a[0] in ("pa", "pb") or b[0] in ("pa", "pb")) else 2.0
-        op("V", lambda g, T: g.vector.tensor_tensor(ap(T, o), ap(T, a), ap(T, b), alu), [o], [a, b], 60 + max(30, two * size(o)))
+        op("V", lambda g, T: g.vector.tensor_tensor(ap(T, o), ap(T, a), ap(T, b), alu), [o], [a, b], ("plain", two * size(o)))
 
     def scan(o, a, b, init, o0, o1):
         op("V", lambda g, T: g.vector.tensor_tensor_scan(ap(T, o), ap(T, a), ap(T, b), init, o0, o1), [o], [a, b],
-           60 + size(o) * (0.5 if narrow(o, a, b) else 1.0))
+           ("plain", size(o) * (0.5 if narrow(o, a, b) else 1.0)))
 
     def fill(o, c):
-        op("V", lambda g, T: g.vector.memset(ap(T, o), c), [o], [], 60 + 0.5 * size(o))
+        op("V", lambda g, T: g.vector.memset(ap(T, o), c), [o], [], ("plain", 0.5 * size(o)))
 
     def tr(o, i):
         op("V", lambda g, T: g.vector.transpose(ap(T, o), ap(T, i)), [o], [i], vcost(o, i))
 
     def quant(c, s, i):
-        op("V", lambda g, T: g.vector.quantize_mx(ap(T, c), ap(T, s), ap(T, i)), [c, s], [i], 30 + 0.27 * size(i))
+        op("V", lambda g, T: g.vector.quantize_mx(ap(T, c), ap(T, s), ap(T, i)), [c, s], [i], ("fixed", 20 + 0.27 * size(i)))
 
     def act(o, i, f, bias=None, scale=None, acc=None):
         def fn(g, T):
@@ -154,7 +158,7 @@ def build():
             if acc is not None:
                 kw["accum_out"] = ap(T, acc)
             return g.scalar.activation(ap(T, o), ap(T, i), f, **kw)
-        op("S", fn, [o] + ([acc] if acc else []), [i, bias], 78 + (1.55 if i[0] == "@" else 1.0) * size(o) + (25 if acc else 0))
+        op("S", fn, [o] + ([acc] if acc else []), [i, bias], ("gather" if i[0] == "@" else "plain", size(o) + (25 if acc else 0)))
 
     def affine(o, i, scale, bias):
         act(o, i, ACT.Identity, bias=bias, scale=scale)
@@ -167,24 +171,25 @@ def build():
 
     def mx(o, wc, ws, xc, xs, start=True, stop=True, grp=None):
         op("P", lambda g, T: g.tensor.matmul_mx(ap(T, o), ap(T, wc), ap(T, ws), ap(T, xc), ap(T, xs), start, stop),
-           [o], [wc, ws, xc, xs], 40 + 0.7 * (size(xc) + 16), grp=grp)
+           [o], [wc, ws, xc, xs], ("product", size(xc) + 16), grp=grp)
 
     def select(o, i, pat, alu, base, cm):
-        op("G", lambda g, T: g.affine_select(ap(T, o), ap(T, i), pat, alu, 0.0, base, cm), [o], [i], 200 + 2 * size(o))
+        op("G", lambda g, T: g.affine_select(ap(T, o), ap(T, i), pat, alu, 0.0, base, cm), [o], [i], ("fixed", 200 + 2 * size(o)))
 
     def iota(o, pat, base, cm=0):
         small = SCRATCH[o[0]][2] != I32
         if small:
-            op("G", lambda g, T: g.iota(ap(T, o), pat, base, cm, allow_small_or_imprecise_dtypes=True), [o], [], 160 + 2 * size(o))
+            op("G", lambda g, T: g.iota(ap(T, o), pat, base, cm, allow_small_or_imprecise_dtypes=True), [o], [],
+               ("fixed", 160 + 2 * size(o)))
         else:
-            op("G", lambda g, T: g.iota(ap(T, o), pat, base, cm), [o], [], 160 + 2 * size(o))
+            op("G", lambda g, T: g.iota(ap(T, o), pat, base, cm), [o], [], ("fixed", 160 + 2 * size(o)))
 
     def dma(q, sem, fo, fi, w, r, lat):
         def fn(g, T):
             return (g.sync if q == "Y" else g.scalar).dma_start(fo(T), fi(T))
-        op(q, fn, w, r, 80, sem=sem, inc=16, lat=lat)
+        op(q, fn, w, r, ("fixed", 80), sem=sem, inc=16, lat=lat)
 
-    def mv(sem, o, i, lat=2200, q="Y"):
+    def mv(sem, o, i, lat=MOVE, q="Y"):
         dma(q, sem, lambda T: ap(T, o), lambda T: ap(T, i), [o], [i], lat)
 
     def u8(x):
@@ -220,18 +225,19 @@ def build():
     iota(v("ck", 22, 46), [[1, 24]], 0)
     ts(ci(5), ci(1), 2, None, ALU.logical_shift_right)
     copy(cf(8), ci(5))
-    ts(cf(9), cf(8), 1024.0, -1.0 - 3072.0, ALU.mult, ALU.add)
-    ts(cf(10), cf(9), 1.0, None, ALU.add)
+    affine(cf(9), cf(8), 1024.0, -1.0 - 3072.0)
+    affine(cf(10), cf(8), 1024.0, -3072.0)
     iota(v("c16"), [[0, 36], [1, 16]], 0)
-    iota(v("c4"), [[0, 25], [1, 4]], 0)
-    ts(v("ky"), v("c4"), cf(8), None, ALU.not_equal)
-    affine(v("dy"), v("ky", 0, 96), 5120.0, -4096.0)
+    iota(v("c4"), [[0, 26], [1, 4]], 0)
+    ts(v("c4"), v("c4"), cf(8), None, ALU.not_equal)
+    affine(v("dy"), v("c4", 0, 96), 5120.0, -4096.0)
     iota(v("ck", 0, 8), [[0, 8]], 0)
     iota(v("ck", 8, 10), [[1, 2]], 1)
     iota(v("ck", 64, 92), [[16, 28]], 0)
-    o_b, o_z, o_t, o_pi, o_u = v("cu", 0, 4), v("cu", 4, 10), v("cu", 64, 92), v("cu", 22, 46), v("cu", 46, 62)
+    o_b, o_z, o_t, o_pi, o_u = v("cu", 0, 1), v("cu", 4, 10), v("cu", 64, 92), v("cu", 22, 46), v("cu", 46, 62)
+    o_q = v("cu", 96, 120)
     copy(o_u, v("ck", 46, 62))
-    ts(o_b, v("ck", 0, 4), cf(4), None, ALU.add)
+    copy(o_b, cf(4))
     ts(o_z, v("ck", 4, 10), cf(5), None, ALU.add)
     act(v("cl", 160, 188), v("ck", 64, 92), ACT.Identity, bias=cf(0))
     ts(v("ci", 16, 44), v("cl", 160, 188), -13.5, 1.0 / 28, ALU.add, ALU.mult)
@@ -245,33 +251,55 @@ def build():
     ts(c_j4, c_j, 4.0, -960.0, ALU.mult, ALU.add)
     ts(c_pf, v("ck", 22, 46), cf(7), 1.0 / 512, ALU.add, ALU.mult)
     ts(c_p448, v("ck", 22, 46), cf(7), float(M), ALU.add, ALU.add)
+    ts(v("ci", 48, 72), c_j, -11.5, 1.0 / 24, ALU.add, ALU.mult)
+    ts(v("cl", 256, 280), v("ci", 48, 72), -383.0, None, ALU.mult)
+    affine(v("cl", 280, 304), c_j, 16.0, 0.0)
+    tt(v("cl", 304, 328), v("cl", 256, 280), v("cl", 280, 304), ALU.add)
+    copy(o_q, v("cl", 304, 328))
     ts(v("c16"), v("c16"), cf(0), None, ALU.not_equal)
     affine(v("md"), v("c16", 0, P), -2 * BIG, BIG)
     affine(v("r0"), v("c16"), 2 * BIG, -BIG)
     iota(v("j4"), [[4, P]], -960)
+    for x in (v("roo", 0, 16), v("tto", 2 * K + 32)):
+        iota(x, [[0, size(x)]], 0)
+    iota(v("ks", P), [[0, 16]], 1000)
+    iota(v("page", CP, CP + P), [[1, P]], 0)
+    late[0] = True
     iota(v("cz", 0, 64), [[1, 4], [0, 16]], 960)
     iota(v("cz", 64, 96), [[0, 32]], 192)
     iota(v("ones"), [[0, M]], 1)
+    iota(v("pir"), [[1, 24], [24, 16]], 0)
+    for lo in (0, 416):
+        iota(v("tg", lo, lo + 416), [[0, 416]], DUM - AO)
+    for lo in range(0, END, P):
+        hi = min(lo + P, END)
+        if lo != CP:
+            iota(v("page", lo, hi), [[1, hi - lo]], lo - CP)
     fill(v("zer"), 0.0)
     for o in range(2):
         gaps = [(0, LEAD)] + [(LEAD + PITCH * m - 4, LEAD + PITCH * m) for m in range(1, NF)] + [(LEAD + PITCH * NF - 4, WORDS)]
         for lo, hi in gaps:
             act(v("fl%d" % o, 4 * lo, 4 * hi), v("zer", 0, 4 * (hi - lo)), ACT.Copy)
-    for x in (v("roo", 0, 16), v("roa", 0, 16), v("tto", 2 * K + 32), v("tta", 2 * A + 32), v("keep"), v("rj0"), v("rj1"), v("rj2")):
+    for x in (v("roa", 0, 16), v("tta", 2 * A + 32), v("keep", 0, 1), v("pk", A), v("rj2"), v("pz", 2 * A)):
         iota(x, [[0, size(x)]], 0)
     for r in range(R):
-        for lo in range(0, ZS[r] + L, 320):
-            hi = min(lo + 320, ZS[r] + L)
-            iota(v("w%d" % r, lo, hi), [[0, hi - lo]], 0)
+        for lo, n in [(DUM, 16), (ZS[r], L)] + [(ZS[s] + M, L) for s in range(r)]:
+            iota(v("w%d" % r, lo, lo + n), [[0, n]], 0)
         iota(v("w%d" % r, ZS[r] + L, ZS[r] + L + K), [[0, K]], 2)
-    iota(v("bt", 4 * K, 512), [[0, 128]], 0)
+        iota(v("cod", ZS[r], ZS[r] + L + K), [[0, L + K]], 1 + 2 * r)
+        iota(v("cod", ZS[r] + L + K, ZS[r] + L + M), [[0, M - K]], 2 + 2 * r)
+    for lo in range(0, ZS[0], 308):
+        iota(v("cod", lo, lo + 308), [[0, 308]], 0)
+    affine(v("cl", 24, 34), v("cl", 0, 10), 1.0, 0.5)
+    late[0] = False
     iota(v("sr"), [[1, P]], -192)
     iota(v("sa"), [[1, 16], [16, 24]], -192)
     mv("z_sr", v("sr", p=k1), v("sa", p=k1))
-    one, eye = v("wu", 0, 512), v("wu", 512, 1024)
+    one, eye = v("wu"), v("wt", 1536, 2048)
     fill(one, 1.0)
     wcol, whi, wlo = v("wt", 0, 512), v("wt", 512, 1024), v("wt", 1024, 1536)
-    select(wcol, one, [[-16, 8], [0, 64]], ALU.is_ge, 0, 1)
+    fill(wcol, -1.0)
+    select(wcol, wcol, [[-16, 8], [0, 64]], ALU.is_ge, 0, 1)
     select(wcol, wcol, [[16, 8], [0, 64]], ALU.is_ge, 15, -1)
     select(wcol, wcol, [[0, 32], [1, 4], [-1, 4]], ALU.is_equal, 0, 0)
     select(eye, one, [[-1, 128], [0, 4]], ALU.is_equal, 0, 1)
@@ -281,16 +309,11 @@ def build():
     for b in range(4):
         select(v("et", 512 * b, 512 * b + 512), one, [[-4, 128], [-1, 4]], ALU.is_equal, b, 4)
     quant(v("ec"), v("es"), v("et"))
-    ts(v("d0"), v("ones"), cf(2), None, ALU.mult)
-    iota(v("pir"), [[1, 24], [24, 16]], 0)
-    iota(v("ks"), [[0, 400]], 1000)
-    iota(v("tg"), [[0, 832]], DUM - AO)
-    for lo in range(0, END, 394):
-        iota(v("page", lo, lo + 394), [[1, 394]], lo - CP)
+    act(v("d0"), v("ones"), ACT.Identity, bias=cf(2), scale=0.0)
 
     quant(v("uc"), v("us"), v("ut"))
     op("V", lambda g, T: g.vector.tensor_copy(ap(T, v("u2c")).bitcast(dt.uint32), ap(T, v("uc")).bitcast(dt.uint32).indirect(ap(T, o_u))),
-       [v("u2c")], [v("uc"), o_u], 60 + 1.55 * 256)
+       [v("u2c")], [v("uc"), o_u], ("gather", 256))
     act(v("u2s"), ind(v("us"), o_u), ACT.Copy)
 
     for b in range(4):
@@ -308,30 +331,25 @@ def build():
     quant(v("vc"), v("vs"), v("vt"))
 
     def classes():
-        tq = TQ[0]
         for t in range(24):
-            if t < tq:
-                act(v("jq", P * (t % NROT), P * (t % NROT) + P), v("kr"), ACT.Sign, bias=v("kq", t, t + 1), scale=-1.0,
-                    acc=v("st", 216 + t, 217 + t))
-            else:
-                z, y = P * (t % 2), 192 * (t - tq)
-                ts(v("fq", z, z + P), v("kr"), v("kq", t, t + 1), None, ALU.is_lt)
-                scan(v("sq", y, y + 192), v("fq", z, z + 192), v("fq", z + 192, z + P), -192.0, ALU.add, ALU.add)
+            act(v("jq", P * (t % NROT), P * (t % NROT) + P), v("kr"), ACT.Sign, bias=v("kq", t, t + 1), scale=-1.0,
+                acc=v("st", 216 + t, 217 + t))
         act(v("kn"), ind(v("kr"), o_pi), ACT.Copy)
+        mv("s_j", v("kn", p=k1), v("page", CP, CP + P, p=k1))
         q_u = v("lu0", 384, 408)
-        ts(v("se", 0, tq), v("st", 216, 216 + tq), 383.0 + 2 * ZQ, 0.5, ALU.add, ALU.mult)
-        if tq < 24:
-            ts(v("se", tq, 24), v("sq", 191, 192 * (24 - tq), 192), 192.0 + ZQ, None, ALU.add)
-        ts(q_u, v("se", 0, 24), -float(ZQ), None, ALU.add)
+        ts(q_u, v("st", 216, 240), 0.5, 191.5, ALU.mult, ALU.add)
         ts(v("se", 24, 48), v("ptl"), float(CP), None, ALU.add)
         copy(ind(v("ks", 0, P), q_u), v("kn"))
+        act(v("tr"), ind(v("ks", 0, P), o_q), ACT.Copy)
+        mv("s_g", v("se", 0, 24), v("tr", p=k1))
+        copy(v("lv", 0, 24), v("se", 0, 24))
         mv("s_k", v("kl", 0, 24), v("ks", 0, P, p=k0))
         mv("s_k", v("kl", 24, 48), v("ks", 1, P + 1, p=k0))
-        ts(v("st", 240, 288), v("kl"), -0.5 + 1.0 / 1024, None, ALU.add)
-        copy(v("sti", 0, 48), v("st", 240, 288))
+        ts(v("sti", 0, 48), v("kl"), -0.5 + 1.0 / 1024, None, ALU.add)
         tt(v("sb", 0, 24), v("sti", 0, 24), v("sti", 24, 48), ALU.is_equal)
-        mv("s_e", v("keep", 1, P + 1, p=k0), v("sb", 0, 24))
-        mv("s_e", v("keep", 1, P + 1, p=k1), v("sb", 0, 24))
+        copy(v("lv", 104, 128), v("sb", 0, 24))
+        act(v("pn"), ind(v("page", CP, CP + 8), v("lv", 104, 128)), ACT.Copy)
+        act(v("keep", 1, P + 1), ind(v("pn"), o_q), ACT.Copy)
         ts(v("sti", 48, 72), v("sti", 0, 24), 15, None, ALU.bitwise_and)
         ts(v("sti", 72, 96), v("sti", 0, 24), 4, None, ALU.logical_shift_right)
         ts(v("st", 240, 264), v("sti", 48, 72), 28.0, None, ALU.mult)
@@ -357,27 +375,26 @@ def build():
 
         def at(m):
             return LEAD + PITCH * (NF - 1 - m)
-        views = [(at(m), 0) for m in range(NF)] + [(at(m) + 4 * m, k) for m in range(NF + 1) for k in (1, 2)]
+        views = [(at(m), 0) for m in range(NF)] + [(at(m) + 4 * m + d, k) for m in range(NF + 1) for k, d in ((1, 0), (2, 4), (3, 0))]
         views.sort()
-        kinds = [[e for e in views if e[1] == k] for k in range(3)]
-        bank = [("pb", 0) if o == 0 else ("pa", 0), ("pa", 1024), ("pa", 1536)]
+        kinds = [[e for e in views if e[1] // 3 == k] for k in range(2)]
+        bank = [("pa", 1024), ("pa", 1536)] if o == 0 else [("pb", 1024), ("pb", 1536)]
         m, done = NF, LEAD
         for n in CHUNKS:
             for m in range(m - 1, m - 1 - n, -1):
                 tt(v(fl, 4 * at(m), 4 * at(m) + P), row, v(hx, L - 16 * m, L + P - 16 * m), ALU.is_gt)
-            lo, hi = done, done + PITCH * n
+            lo, hi = done, max(done + PITCH * n, done + 128)
             if r == 0:
                 lo, hi = (0 if lo == LEAD else lo), (WORDS if m == 0 else hi)
             quant(v(fc, lo, hi), v(fs, lo, hi), v(fl, 4 * lo, 4 * hi))
             done += PITCH * n
             while views and (m == 0 or views[0][0] + 128 <= done):
                 a, k = e = views.pop(0)
-                mx(v(bank[k][0], bank[k][1], bank[k][1] + 128), v("sumc", 128 * k, 128 * k + 128), v("sums", 128 * k, 128 * k + 128),
-                   v(fc, a, a + 128), v(fs, a, a + 128), e == kinds[k][0], e == kinds[k][-1], (r, o, k))
-        act(v("sy", 0, 100), v("pa", 1024, 1124), ACT.Copy)
-        tt(v("sy", 104, 204), v("sy", 0, 100), v("pa", 1537, 1637), ALU.add)
-        scan(v("sy", 208, 308), v("ky"), v("sy", 104, 204), 0.0, ALU.mult, ALU.add)
-        tt(v("sy", 312, 408), v("sy", 211, 307), v(bank[0][0], bank[0][1], bank[0][1] + 96), ALU.subtract)
+                y = k // 3
+                mx(v(bank[y][0], bank[y][1], bank[y][1] + 128), v("sumc", 128 * k, 128 * k + 128), v("sums", 128 * k, 128 * k + 128),
+                   v(fc, a, a + 128), v(fs, a, a + 128), e == kinds[y][0], e == kinds[y][-1], (r, o, y))
+        scan(v("sy", 208, 308), v("c4", 3, 103), v(bank[1][0], bank[1][1], bank[1][1] + 100), 0.0, ALU.mult, ALU.add)
+        tt(v("sy", 312, 408), v("sy", 211, 307), v(bank[0][0], bank[0][1], bank[0][1] + 96), ALU.add)
         scan(v("sy", 416, 512), v("dy"), v("sy", 312, 408), 0.0, ALU.add, ALU.max)
         tt(v(lf, out, out + 24), v("sy", 419, 512, 4), v("gc", g0, g0 + 24), ALU.add)
 
@@ -391,25 +408,26 @@ def build():
         def f(i, n=24, lf=lf):
             return v(lf, 192 + 24 * i, 192 + 24 * i + n)
         ro, ra = f(0), f(1)
-        quant(v("qc"), v("qs"), v(x, 0, 4 * P))
+        bc, bs, lc, ls = v("bc%d" % r), v("bs%d" % r), v("lc%d" % r), v("ls%d" % r)
+        quant(bc, bs, v(x, 0, 4 * P))
         for i in range(2):
             c = 128 * i
-            mx(v("pa", 512 * i, 512 * i + P), v("u2c", c, c + 128), v("u2s", c, c + 128), v("qc"), v("qs"))
+            mx(v("pa", 512 * i, 512 * i + P), v("u2c", c, c + 128), v("u2s", c, c + 128), bc, bs)
+        op("G", ("send", r, 0), [lc], [bc], ("send", 1), sem="arr%d" % r, inc=8, lat=1.6 * SEND)
+        op("G", ("send", r, 1), [ls], [bs], ("send", 1), sem="arr%d" % r, inc=8, lat=1.6 * SEND)
+        for b in range(4):
+            at = 512 * (b % 2)
+            mx(v("pb", at, at + P), v("ec", 128 * b, 128 * b + 128), v("es", 128 * b, 128 * b + 128), lc, ls)
+            act(v("df", P * b, P * b + P), v("pb", at, at + P), ACT.Copy)
         rank(r, 0, 192)
         ts(v(lu, 0, 24), ro, 192.0, None, ALU.add)
         copy(ind(v("roo", 16, 400), v(lu, 0, 24)), v("j4"))
         to_list("roo", K, "tto")
-        tt(v(lf, 672, 736), ind(v("tto"), o_b), v("cz", 0, 64), ALU.add)
-        copy(v(lu, 48, 112), v(lf, 672, 736))
+        ts(v(lu, 48, 64), ind(v("tto"), o_b), 0.25, 240.0, ALU.mult, ALU.add)
+        won = v("ll", 16 * r, 16 * r + 6)
+        op("G", ("send", r, 2), [won], [v(lu, 48, 54)], ("send", 1), sem="arl%d" % r, inc=8, lat=SEND)
         for b in range(4):
-            gather(GB[r][b], v("bt", b, 4 * K, 4), ind(v(x, 0, 4 * P), v(lu, 48 + 16 * b, 54 + 16 * b)))
-        bc, bs, lc, ls = v("bc%d" % r), v("bs%d" % r), v("lc%d" % r), v("ls%d" % r)
-        quant(bc, bs, v("bt"))
-        op("G", ("send", r, 0), [lc], [bc], 400, sem="arr%d" % r, inc=4, lat=4500)
-        op("G", ("send", r, 1), [ls], [bs], 400, sem="arr%d" % r, inc=4, lat=4500)
-        for b in range(4):
-            mx(v("pb", 512 * b, 512 * b + 128), v("ec", 128 * b, 128 * b + 128), v("es", 128 * b, 128 * b + 128), lc, ls)
-            gather(GD[r][b], v(x, 4 * P + b, 4 * (P + K), 4), v("pb", 512 * b, 512 * b + K))
+            gather(GD[r][b], v(x, 4 * P + b, 4 * (P + K), 4), ind(v("df", P * b, P * b + P), won))
         h, u_, km, k2 = f(2), f(3), f(5), f(4)
         s4 = v("s4%d" % r, 0, 24)
         act(f(6), ro, ACT.Sign, bias=-95.5)
@@ -419,7 +437,7 @@ def build():
         tt(km, k2, h, ALU.add)
         affine(f(7), km, 4.0, 4.0 * P - 960.0)
         tt(s4, f(7), c_j4, ALU.max)
-        mv("r_s%d" % r, v("sr", p=k0), s4)
+        mv("r_s%d" % r, v("sr", p=k0), s4, 1.5 * MOVE)
         act(v("nr"), ind(v("sr"), o_pi), ACT.Copy)
         rank(r, 1, 216)
         ts(v(lu, 24, 48), ra, 192.0, None, ALU.add)
@@ -435,7 +453,8 @@ def build():
         tt(f(9), f(15), f(8), ALU.subtract)
         tt(f(10), f(9), s4, ALU.max)
         for b in range(4):
-            ts(v(lu, 208 + 32 * b, 232 + 32 * b), f(10), 960.0 + b, None, ALU.add)
+            affine(v(lf, 24 * b, 24 * b + 24), f(10), 1.0, 960.0 + b)
+        copy(v(lu, 208, 304), v(lf, 0, 96))
         for b in range(4):
             mx(v("pb", 512 * b, 512 * b + A), v("wq", 128 * b, 128 * b + 128), v("wp", 128 * b, 128 * b + 128), v("zc"), v("zs"))
             act(v("rb", b, 4 * A, 4), v("pb", 512 * b, 512 * b + A), ACT.Relu, scale=0.03125)
@@ -446,24 +465,41 @@ def build():
         nc = 1 if r + 1 < R else 3
         for c in range(nc):
             for b in range(4):
-                lo, n = 208 + 32 * b + 8 * c, 24 // nc
+                lo, n = 208 + 24 * b + 8 * c, 24 // nc
                 gather(GF[r][b], v(xn, 512 * c + b, 512 * c + 64 * n, 4), ind(v(x), v(lu, lo, lo + n)))
 
         if r == 0:
             classes()
-        affine(f(13), k2, 1.0, float(ZS[r]))
         affine(f(14), km, 1.0, float(ZS[r] + L))
-        tt(v("se"), v("se"), f(13, 48), ALU.max)
-        copy(v(lu, 336, 384), v("se"))
-        copy(ind(v(w), v(lu, 336, 360)), v("ones", 0, P))
+        tt(v("se", 24, 48), v("se", 24, 48), f(14), ALU.max)
+        copy(v(lu, 360, 384), v("se", 24, 48))
+        kind = v("cr", 0, P)
+        act(kind, ind(v("cod"), v(lu, 360, 384)), ACT.Copy)
+        act(v(w, ZQ, ZQ + P), ind(kind, v("lv", 0, 24)), ACT.Relu, bias=1.0, scale=-1.0)
         scan(v(w, AO, AO + P), v("keep", 0, P), v(w, ZQ, ZQ + P), 0.0, ALU.mult, ALU.add)
         for s in range(r):
+            act(v(w, ZS[s], ZS[s] + L), ind(kind, v("lv", 44 + 24 * s, 56 + 24 * s)), ACT.Relu, bias=2.0 + 2 * s, scale=-1.0)
             tt(v(w, ZS[s] + L, ZS[s] + L + K), v(w, ZS[s] + K, ZS[s] + L), v(w, ZS[s], ZS[s] + K), ALU.add)
+            act(v("pz", A, 2 * A), ind(kind, v("lu%d" % s, 176, 186)), ACT.Relu, bias=3.0 + 2 * s, scale=-1.0)
+            act(v(w, ZS[s] + L + K, ZS[s] + L + K + A), ind(v("pz", A, 2 * A + 16), v("lv", 80 + 16 * s, 90 + 16 * s)), ACT.Copy)
         act(v(w, CP, CP + M), ind(v(w, AO, ZS[r]), v(lu, 384, 412)), ACT.Copy)
         act(v("mr"), ind(v(w), v(lu, 360, 384)), ACT.Sign, bias=-1.5)
         act(v("mk"), ind(v("mr"), v(lu, 176, 186)), ACT.Relu)
-        scan(v("pk"), v("d0", 0, A), v("mk"), 0.0, ALU.mult, ALU.add)
-        copy(ind(v("rj%d" % r), v(lu, 192, 202)), v("pk"))
+        scan(v("pk", 0, A), v("d0", 0, A), v("mk"), 0.0, ALU.mult, ALU.add)
+        if r + 1 < R:
+            act(v("pn"), ind(v("pk"), v(lu, 24, 48)), ACT.Copy)
+            act(v("rj%d" % r), ind(v("pn"), o_q), ACT.Copy)
+            act(v("cr", P, 2 * P), ind(v("roo", 16, 400), o_q), ACT.Copy)
+            mv("r_l%d" % r, v("pj%d" % r, 112, 136), v("cr", P, 2 * P, p=k0))
+            affine(f(13), v("pj%d" % r, 112, 136), 0.25, 240.0)
+            copy(v("lv", 32 + 24 * r, 56 + 24 * r), f(13))
+            scan(v("pz", 0, A), v("ones", 0, A), v("mk"), 0.0, ALU.mult, ALU.add)
+            for t in range(10):
+                act(v("jq", P * (t % NROT), P * (t % NROT) + A), v("pz", 0, A), ACT.Sign, bias=v("cl", 24 + t, 25 + t), scale=-1.0,
+                    acc=v("st", t, t + 1))
+            ts(v("lv", 80 + 16 * r, 90 + 16 * r), v("st", 0, 10), 0.5, A / 2, ALU.mult, ALU.add)
+        else:
+            copy(ind(v("rj%d" % r), v(lu, 192, 202)), v("pk", 0, A))
         pj = "pj%d" % r
         mv("r_p%d" % r, v(pj, 0, 24), v("rj%d" % r, p=k0))
         mv("r_p%d" % r, v(pj, 24, 48), v("rj%d" % r, p=k1))
@@ -481,8 +517,6 @@ def build():
         copy(v(nu, n0, n0 + 28), v("tag", 0, 28))
         affine(f(12), v(pj, 24, 48), FAR, float(ZS[r] + L + K - 1) - FAR)
         tt(f(11), f(12), v(pj, 0, 24), ALU.add)
-        if r + 1 < R:
-            tt(v("se", 0, 24), v("se", 0, 24), f(11), ALU.max)
         tt(v("se", 24, 48), v("se", 24, 48), f(11), ALU.max)
 
     copy(ind(v("page", AO, END), v("stu", 0, 28)), v("page", CP, CP + M))
@@ -539,22 +573,41 @@ def plan():
                 dep.update(groups[ops[j]["sem"]])
         dep.discard(i)
         o["dep"] = sorted(dep)
+        o["ix"] = i
+    first = [o for o in ops if o["sem"] == "arl0"][0]["dep"]
+    for o in ops:
+        if o["late"]:
+            o["dep"] = sorted(set(o["dep"] + first))
     succ = [[] for _ in range(n)]
     for i, o in enumerate(ops):
         for j in o["dep"]:
             succ[j].append(i)
-    wake = LOOK[2]
-    prio = [0.0] * n
-    for i in range(n - 1, -1, -1):
-        prio[i] = ops[i]["cost"] + ops[i]["lat"] + ops[i]["early"] + max([prio[s] + wake for s in succ[i]] + [0.0])
-    x = SEED[0]
-    for i in range(n):
-        x = (x * 1103515245 + 12345) % 2147483648
-        prio[i] += SEED[1] * (x / 2147483648.0)
+    figures = []
+    for fix, least, wake, scatter, gather, product, slow, issue in CASES:
+        cost = []
+        for o in ops:
+            k, m = o["cost"]
+            extra = 18.0 if o["eng"] == "S" else 0.0
+            cost.append({"plain": extra + fix + max(least, m), "gather": extra + 60 + gather * m, "scatter": 60 + scatter * m,
+                         "product": 30 + product * m, "fixed": m, "send": issue}[k])
+        figures.append((cost, [o["lat"] * slow for o in ops], wake))
 
-    def schedule(prio, before, after, back):
+    def replay(order, case):
+        cost, lat, wake = figures[case]
+        free, end = {e: 0.0 for e in "VSPGY"}, [0.0] * n
+        for i in order:
+            o = ops[i]
+            t = free[o["eng"]]
+            for j in o["dep"]:
+                t = max(t, end[j] + (0.0 if o["grp"] and o["grp"] == ops[j]["grp"] else wake))
+            free[o["eng"]] = t + cost[i]
+            end[i] = t + cost[i] + lat[i]
+        return max(end)
+
+    def schedule(prio, before, after, back, case):
+        cost, lat, wake = figures[case]
         left = [len(x) for x in before]
-        ready_at = [ops[i]["lat"] if back else 0.0 for i in range(n)]
+        ready_at = [lat[i] if back else 0.0 for i in range(n)]
         ready = {e: [] for e in "VSPGY"}
         for i in range(n):
             if left[i] == 0:
@@ -571,32 +624,48 @@ def plan():
             t, e = best
             top = max(ready[e], key=lambda i: prio[i])
             i = max([i for i in ready[e] if ready_at[i] <= t], key=lambda i: prio[i])
-            if ready_at[top] > t and ready_at[top] - t < LOOK[0] * ops[i]["cost"] and prio[top] > prio[i] + LOOK[1]:
+            if ready_at[top] > t and ready_at[top] - t < LOOK[0] * cost[i] and prio[top] > prio[i] + LOOK[1]:
                 i, t = top, ready_at[top]
             ready[e].remove(i)
             start[i] = t
-            free[e] = t + ops[i]["cost"]
-            end[i] = free[e] + (0.0 if back else ops[i]["lat"])
+            free[e] = t + cost[i]
+            end[i] = free[e] + (0.0 if back else lat[i])
             order.append(i)
             for s in after[i]:
                 gap = 0.0 if ops[i]["grp"] and ops[i]["grp"] == ops[s]["grp"] else wake
-                ready_at[s] = max(ready_at[s], end[i] + gap + (ops[s]["lat"] if back else 0.0))
+                ready_at[s] = max(ready_at[s], end[i] + gap + (lat[s] if back else 0.0))
                 left[s] -= 1
                 if left[s] == 0:
                     ready[ops[s]["eng"]].append(s)
         return order, start, end
 
     pred = [o["dep"] for o in ops]
-    kept = None
-    for turn in range(TURNS[0]):
-        order, start, end = schedule(prio, pred, succ, False)
-        if kept is None or max(end) < kept[0]:
-            kept = (max(end), order, start, end)
-        if turn + 1 < TURNS[0]:
-            prio = schedule(end, succ, pred, True)[2]
+    kept, x = None, SEED[0]
+    for case in range(len(CASES)):
+        cost, lat, wake = figures[case]
+        prio = [0.0] * n
+        for i in range(n - 1, -1, -1):
+            prio[i] = cost[i] + lat[i] + ops[i]["early"] + max([prio[s] + wake for s in succ[i]] + [0.0])
+        local = None
+        for turn in range(TURNS[0]):
+            order, start, end = schedule(prio, pred, succ, False, case)
+            times = [replay(order, c) for c in range(WEIGHED)]
+            if kept is None or sum(times) < kept[0]:
+                kept = (sum(times), order, start, end, times, case)
+            if local is None or sum(times) < local:
+                local = sum(times)
+                prio = base = schedule(end, succ, pred, True, case)[2]
+            else:
+                prio = []
+                for i in range(n):
+                    x = (x * 1103515245 + 12345) % 2147483648
+                    prio.append(base[i] + SEED[1] * (x / 2147483648.0))
+                if turn % 2:
+                    prio = schedule(schedule(prio, pred, succ, False, case)[2], succ, pred, True, case)[2]
     order = kept[1]
     for i in order:
-        ops[i]["start"], ops[i]["done"] = kept[2][i], kept[3][i]
+        ops[i]["start"], ops[i]["done"], ops[i]["cost"] = kept[2][i], kept[3][i], figures[kept[5]][0][i]
+    ops[order[0]]["times"] = kept[4]
     count = {}
     for i in order:
         o = ops[i]
@@ -631,7 +700,7 @@ def rank_program(g, core, T, topo):
     nxt = T.cores[(rank + 1) % len(T.cores)]
     rid, pid = topo.addr(nxt)[:2]
     eng = topo.engines(core, nxt)
-    masks = [sum(1 << e for e in eng[4 * i:4 * i + 4]) for i in range(2)]
+    mask = sum(1 << e for e in eng[:8])
     queue = {"V": g.vector, "S": g.scalar, "P": g.tensor, "G": g, "Y": g.sync}
     for o in PLAN:
         q = queue[o["eng"]]
@@ -641,9 +710,9 @@ def rank_program(g, core, T, topo):
             src, dst = ap(T, o["r"][0]), ap(T, o["w"][0])
             if o["fn"][2] == 0:
                 src, dst = src.bitcast(dt.uint8), dst.bitcast(dt.uint8)
-            g.remote_dma(dst, src, T.sem[o["sem"]], T.sem["snt"], pid, rid, masks[o["fn"][2]])
+            g.remote_dma(dst, src, T.sem[o["sem"]], T.sem["snt"], pid, rid, mask)
         else:
             o["fn"](g, T).then_inc(T.sem[o["at"][0]], o["inc"])
     for s in sorted(COUNT):
         g.wait_ge(T.sem[s], COUNT[s])
-    g.wait_ge(T.sem["snt"], 8 * R)
+    g.wait_ge(T.sem["snt"], 24 * R)

from concourse.mybir import dt, AluOpType, ActivationFunctionType

ALU = AluOpType
ACT = ActivationFunctionType
M, P, K, L, A, R = 448, 384, 96, 192, 160, 3
BIG = 4.0e29
FAR = 4096.0
STEP = 2.0 ** -24 * (1.0 + 2.0 ** -6)
TINY = 2.0 ** -125
ZQ, CP, AO, DUM = 0, 384, 832, 1216
ZS = [1232, 1872, 2512]
END = 3152
ZW = 208
NF, LEAD, PITCH, WORDS = 12, 52, 100, 1284
CHUNKS = [3, 3, 2, 2, 2]
GZ = ["SVSV", "SVSV", "SVSV"]
GF = ["SVSS", "SVSS", "SVSS"]
GD = ["SSSS", "SSSS", "SSSS"]
HS = [1, 1, 1]
LOOK = [0.3, 1000.0]
SEED = [2, 1500.0]
TURNS = [24]
SEND, MOVE = 5000.0, 2500.0
CASES = [(55.0, 20.0, 90.0, 3.1, 1.5, 0.6, 1.15, 800.0), (45.0, 20.0, 70.0, 2.5, 1.8, 0.5, 1.3, 1200.0),
         (60.0, 20.0, 120.0, 4.5, 1.2, 0.8, 1.0, 600.0), (60.0, 30.0, 70.0, 3.7, 1.55, 0.7, 1.0, 400.0),
         (55.0, 20.0, 90.0, 3.1, 1.6, 0.8, 1.6, 1400.0), (55.0, 20.0, 110.0, 3.1, 1.7, 0.9, 1.4, 1000.0)]
WEIGHED = 4
NROT = 4

BF, F32, I32, U16, CODE, U8 = "bfloat16", "float32", "int32", "uint16", "float8_e4m3fn_x4", "uint8"
SCRATCH = {}


def _sb(name, n, d):
    SCRATCH[name] = ("sbuf", [128, n], d)


for _n, _w, _d in [
    ("mm", 4 * M, BF), ("ut", 512, BF), ("vt", 512, BF), ("ptl", 24, I32),
    ("uc", 128, CODE), ("us", 128, U8), ("u2c", 256, CODE), ("u2s", 256, U8), ("vc", 128, CODE), ("vs", 128, U8),
    ("wq", 512, CODE), ("wp", 512, U8), ("et", 2048, BF), ("ec", 512, CODE), ("es", 512, U8),
    ("x0", 2560, BF), ("x1", 2560, BF), ("x2", 2560, BF), ("x3", 1536, BF),
    ("qc", P, CODE), ("qs", P, U8), ("df", 4 * P, BF), ("ll", 48, U16), ("zt", 640, BF), ("zc", A, CODE), ("zs", A, U8), ("rb", 640, F32),
    ("ci", 80, I32), ("cf", 16, F32), ("ck", 96, F32), ("cu", 128, U16), ("cl", 336, F32),
    ("c16", 576, BF), ("md", P, BF), ("r0", 576, BF), ("c4", 104, BF), ("dy", 96, BF),
    ("wt", 2048, BF), ("wu", 512, BF), ("sumc", 512, CODE), ("sums", 512, U8),
    ("ones", M, BF), ("d0", M, BF),
    ("j4", P, BF), ("sr", P, BF), ("sa", P, BF), ("nr", P, BF), ("pir", P, F32),
    ("cz", 96, F32), ("tg", 832, F32), ("page", END, F32), ("ks", 400, F32), ("kr", P, F32), ("kn", P, F32),
    ("zer", ZW, BF), ("w0", ZS[0] + L + K, BF), ("w1", ZS[1] + L + K, BF), ("w2", ZS[2] + L + K, BF),
    ("keep", 400, BF), ("roo", 416, BF), ("roa", 416, BF), ("pf", M, BF), ("tto", 368, BF), ("tta", 432, BF), ("pp", M, BF),
    ("dx0", 576, F32), ("dx1", 576, F32), ("dl0", L, F32), ("dl1", L, F32), ("hx0", 576, F32), ("hx1", 576, F32),
    ("fl0", 4 * WORDS, BF), ("fl1", 4 * WORDS, BF), ("fc0", WORDS, CODE), ("fc1", WORDS, CODE), ("fs0", WORDS, U8), ("fs1", WORDS, U8),
    ("sy", 512, F32), ("gc", 96, F32), ("jq", NROT * P, BF), ("cod", END, BF), ("cr", 2 * P, BF), ("lv", 128, U16), ("pz", 2 * A + 16, BF),
    ("st", 320, F32), ("kq", 24, F32), ("sti", 128, I32), ("stu", 128, U16), ("kl", 48, F32), ("sb", 32, F32), ("tag", 32, F32),
    ("se", 48, F32), ("fre", M, BF), ("mr", P, BF), ("mk", A, BF), ("pk", P, BF), ("pn", P, BF), ("tr", P, F32), ("yb", P, F32),
]:
    _sb(_n, _w, _d)
for _r in range(R):
    for _n, _w, _d in [("bc", P, CODE), ("bs", P, U8), ("lc", P, CODE), ("ls", P, U8), ("lu", 416, U16), ("lf", 800, F32),
                       ("s4", 32, BF), ("rj", P, BF), ("pj", 136, BF)]:
        _sb("%s%d" % (_n, _r), _w, _d)
SCRATCH["pa"] = ("psum", [128, 2048], F32)
SCRATCH["pb"] = ("psum", [128, 2048], F32)


def v(name, lo=0, hi=None, step=1, p=None):
    return (name, lo, SCRATCH[name][1][1] if hi is None else hi, step, p)


def ind(win, off):
    return ("@", win, off)


def ap(T, x):
    if not isinstance(x, tuple):
        return x
    if x[0] == "@":
        return ap(T, x[1]).indirect(ap(T, x[2]))
    name, lo, hi, step, p = x
    ps = slice(0, 128) if p is None else slice(p[0], p[1], p[2])
    return T[name][ps, lo:hi:step] if step > 1 else T[name][ps, lo:hi]


def size(x):
    if x[0] == "@":
        return 16 * size(x[2])
    return len(range(x[1], x[2], x[3]))


def narrow(*xs):
    return all(SCRATCH[x[0]][2] in (BF, U16) for x in xs)


def parts(xs):
    out = []
    for x in xs:
        if isinstance(x, tuple):
            out += [x[1], x[2]] if x[0] == "@" else [x]
    return out


def build():
    ops = []
    early, late = [0.0], [False]

    def op(eng, fn, w, r, cost, sem=None, inc=1, lat=0.0, grp=None):
        wr, rd = [], parts(r)
        for x in w:
            if x[0] == "@":
                wr.append(x[1])
                rd.append(x[2])
            else:
                wr.append(x)
        ops.append({"eng": eng, "fn": fn, "w": wr, "r": rd, "cost": cost, "sem": sem, "inc": inc, "lat": lat, "early": early[0], "grp": grp,
                    "late": late[0] and eng == "G"})

    def vcost(o, i):
        if o[0] == "@":
            return ("scatter", size(o))
        if i[0] == "@":
            return ("gather", size(o))
        return ("plain", size(o) * (0.5 if narrow(o, i) else 1.0))

    def copy(o, i):
        op("V", lambda g, T: g.vector.tensor_copy(ap(T, o), ap(T, i)), [o], [i], vcost(o, i))

    def ts(o, i, s1, s2, o0, o1=None):
        if o1 is None:
            op("V", lambda g, T: g.vector.tensor_scalar(ap(T, o), ap(T, i), ap(T, s1), None, o0), [o], [i, s1], vcost(o, i))
        else:
            op("V", lambda g, T: g.vector.tensor_scalar(ap(T, o), ap(T, i), ap(T, s1), ap(T, s2), o0, o1), [o], [i, s1, s2], vcost(o, i))

    def tt(o, a, b, alu):
        two = 1.0 if (a[0] in ("pa", "pb") or b[0] in ("pa", "pb")) else 2.0
        op("V", lambda g, T: g.vector.tensor_tensor(ap(T, o), ap(T, a), ap(T, b), alu), [o], [a, b], ("plain", two * size(o)))

    def scan(o, a, b, init, o0, o1):
        op("V", lambda g, T: g.vector.tensor_tensor_scan(ap(T, o), ap(T, a), ap(T, b), init, o0, o1), [o], [a, b],
           ("plain", size(o) * (0.5 if narrow(o, a, b) else 1.0)))

    def fill(o, c):
        op("V", lambda g, T: g.vector.memset(ap(T, o), c), [o], [], ("plain", 0.5 * size(o)))

    def tr(o, i):
        op("V", lambda g, T: g.vector.transpose(ap(T, o), ap(T, i)), [o], [i], vcost(o, i))

    def quant(c, s, i):
        op("V", lambda g, T: g.vector.quantize_mx(ap(T, c), ap(T, s), ap(T, i)), [c, s], [i], ("fixed", 20 + 0.27 * size(i)))

    def act(o, i, f, bias=None, scale=None, acc=None):
        def fn(g, T):
            kw = {}
            if bias is not None:
                kw["bias"] = ap(T, bias)
            if scale is not None:
                kw["scale"] = scale
            if acc is not None:
                kw["accum_out"] = ap(T, acc)
            return g.scalar.activation(ap(T, o), ap(T, i), f, **kw)
        op("S", fn, [o] + ([acc] if acc else []), [i, bias], ("gather" if i[0] == "@" else "plain", size(o) + (25 if acc else 0)))

    def affine(o, i, scale, bias):
        act(o, i, ACT.Identity, bias=bias, scale=scale)

    def gather(eng, o, i):
        if eng == "S":
            act(o, i, ACT.Copy)
        else:
            copy(o, i)

    def mx(o, wc, ws, xc, xs, start=True, stop=True, grp=None):
        op("P", lambda g, T: g.tensor.matmul_mx(ap(T, o), ap(T, wc), ap(T, ws), ap(T, xc), ap(T, xs), start, stop),
           [o], [wc, ws, xc, xs], ("product", size(xc) + 16), grp=grp)

    def select(o, i, pat, alu, base, cm):
        op("G", lambda g, T: g.affine_select(ap(T, o), ap(T, i), pat, alu, 0.0, base, cm), [o], [i], ("fixed", 200 + 2 * size(o)))

    def iota(o, pat, base, cm=0):
        small = SCRATCH[o[0]][2] != I32
        if small:
            op("G", lambda g, T: g.iota(ap(T, o), pat, base, cm, allow_small_or_imprecise_dtypes=True), [o], [],
               ("fixed", 160 + 2 * size(o)))
        else:
            op("G", lambda g, T: g.iota(ap(T, o), pat, base, cm), [o], [], ("fixed", 160 + 2 * size(o)))

    def dma(q, sem, fo, fi, w, r, lat):
        def fn(g, T):
            return (g.sync if q == "Y" else g.scalar).dma_start(fo(T), fi(T))
        op(q, fn, w, r, ("fixed", 80), sem=sem, inc=16, lat=lat)

    def mv(sem, o, i, lat=MOVE, q="Y"):
        dma(q, sem, lambda T: ap(T, o), lambda T: ap(T, i), [o], [i], lat)

    def u8(x):
        return lambda T: ap(T, x).bitcast(dt.uint8)

    k0, k1 = (0, 128, 16), (1, 128, 16)

    early[0] = 3000.0
    dma("Y", "ld_pl", lambda T: ap(T, v("ptl")), lambda T: T.pt[:], [v("ptl")], [], 2200)
    early[0] = 0.0
    dma("Y", "ld_m0", lambda T: ap(T, v("mm", 0, 896)), lambda T: T.m[:, 0:896], [v("mm", 0, 896)], [], 3500)
    dma("S", "ld_m1", lambda T: ap(T, v("mm", 896, 1792)), lambda T: T.m[:, 896:1792], [v("mm", 896, 1792)], [], 3500)
    dma("S", "ld_u", lambda T: ap(T, v("ut")), lambda T: T.u[:], [v("ut")], [], 2600)

    def ci(i):
        return v("ci", i, i + 1)

    def cf(i):
        return v("cf", i, i + 1)
    iota(ci(0), [[0, 1]], 0, 1)
    ts(ci(1), ci(0), 15, None, ALU.bitwise_and)
    ts(ci(2), ci(0), 4, None, ALU.logical_shift_right)
    tt(ci(3), ci(1), ci(2), ALU.add)
    ts(ci(4), ci(3), 1, None, ALU.bitwise_and)
    copy(cf(0), ci(1))
    copy(cf(1), ci(4))
    ts(cf(2), cf(0), 0.0, None, ALU.is_equal)
    ts(cf(3), cf(0), 16.0, None, ALU.mult)
    for i, n in ((4, K), (5, A)):
        ts(cf(i), cf(1), float(n + 16), cf(3), ALU.mult, ALU.add)
    ts(cf(7), cf(0), 24.0, None, ALU.mult)
    iota(v("ck", 46, 62), [[1, 2], [16, 8]], 0)
    iota(v("ck", 22, 46), [[1, 24]], 0)
    ts(ci(5), ci(1), 2, None, ALU.logical_shift_right)
    copy(cf(8), ci(5))
    affine(cf(9), cf(8), 1024.0, -1.0 - 3072.0)
    affine(cf(10), cf(8), 1024.0, -3072.0)
    iota(v("c16"), [[0, 36], [1, 16]], 0)
    iota(v("c4"), [[0, 26], [1, 4]], 0)
    ts(v("c4"), v("c4"), cf(8), None, ALU.not_equal)
    affine(v("dy"), v("c4", 0, 96), 5120.0, -4096.0)
    iota(v("ck", 0, 8), [[0, 8]], 0)
    iota(v("ck", 8, 10), [[1, 2]], 1)
    iota(v("ck", 64, 92), [[16, 28]], 0)
    o_b, o_z, o_t, o_pi, o_u = v("cu", 0, 1), v("cu", 4, 10), v("cu", 64, 92), v("cu", 22, 46), v("cu", 46, 62)
    o_q = v("cu", 96, 120)
    copy(o_u, v("ck", 46, 62))
    copy(o_b, cf(4))
    ts(o_z, v("ck", 4, 10), cf(5), None, ALU.add)
    act(v("cl", 160, 188), v("ck", 64, 92), ACT.Identity, bias=cf(0))
    ts(v("ci", 16, 44), v("cl", 160, 188), -13.5, 1.0 / 28, ALU.add, ALU.mult)
    ts(v("cl", 192, 220), v("ci", 16, 44), -447.0, None, ALU.mult)
    affine(v("cl", 160, 188), v("cl", 160, 188), 16.0, 0.0)
    tt(v("cl", 224, 252), v("cl", 160, 188), v("cl", 192, 220), ALU.add)
    copy(o_t, v("cl", 224, 252))
    ts(o_pi, v("ck", 22, 46), cf(7), None, ALU.add)
    c_j, c_j4, c_pf, c_p448 = v("cl", 0, 24), v("cl", 48, 72), v("cl", 96, 120), v("cl", 120, 144)
    ts(c_j, v("ck", 22, 46), 16.0, cf(0), ALU.mult, ALU.add)
    ts(c_j4, c_j, 4.0, -960.0, ALU.mult, ALU.add)
    ts(c_pf, v("ck", 22, 46), cf(7), 1.0 / 512, ALU.add, ALU.mult)
    ts(c_p448, v("ck", 22, 46), cf(7), float(M), ALU.add, ALU.add)
    ts(v("ci", 48, 72), c_j, -11.5, 1.0 / 24, ALU.add, ALU.mult)
    ts(v("cl", 256, 280), v("ci", 48, 72), -383.0, None, ALU.mult)
    affine(v("cl", 280, 304), c_j, 16.0, 0.0)
    tt(v("cl", 304, 328), v("cl", 256, 280), v("cl", 280, 304), ALU.add)
    copy(o_q, v("cl", 304, 328))
    ts(v("c16"), v("c16"), cf(0), None, ALU.not_equal)
    affine(v("md"), v("c16", 0, P), -2 * BIG, BIG)
    affine(v("r0"), v("c16"), 2 * BIG, -BIG)
    iota(v("j4"), [[4, P]], -960)
    for x in (v("roo", 0, 16), v("tto", 2 * K + 32)):
        iota(x, [[0, size(x)]], 0)
    iota(v("ks", P), [[0, 16]], 1000)
    iota(v("page", CP, CP + P), [[1, P]], 0)
    late[0] = True
    iota(v("cz", 0, 64), [[1, 4], [0, 16]], 960)
    iota(v("cz", 64, 96), [[0, 32]], 192)
    iota(v("ones"), [[0, M]], 1)
    iota(v("pir"), [[1, 24], [24, 16]], 0)
    for lo in (0, 416):
        iota(v("tg", lo, lo + 416), [[0, 416]], DUM - AO)
    for lo in range(0, END, P):
        hi = min(lo + P, END)
        if lo != CP:
            iota(v("page", lo, hi), [[1, hi - lo]], lo - CP)
    fill(v("zer"), 0.0)
    for o in range(2):
        gaps = [(0, LEAD)] + [(LEAD + PITCH * m - 4, LEAD + PITCH * m) for m in range(1, NF)] + [(LEAD + PITCH * NF - 4, WORDS)]
        for lo, hi in gaps:
            act(v("fl%d" % o, 4 * lo, 4 * hi), v("zer", 0, 4 * (hi - lo)), ACT.Copy)
    for x in (v("roa", 0, 16), v("tta", 2 * A + 32), v("keep", 0, 1), v("pk", A), v("rj2"), v("pz", 2 * A)):
        iota(x, [[0, size(x)]], 0)
    for r in range(R):
        for lo, n in [(DUM, 16), (ZS[r], L)] + [(ZS[s] + M, L) for s in range(r)]:
            iota(v("w%d" % r, lo, lo + n), [[0, n]], 0)
        iota(v("w%d" % r, ZS[r] + L, ZS[r] + L + K), [[0, K]], 2)
        iota(v("cod", ZS[r], ZS[r] + L + K), [[0, L + K]], 1 + 2 * r)
        iota(v("cod", ZS[r] + L + K, ZS[r] + L + M), [[0, M - K]], 2 + 2 * r)
    for lo in range(0, ZS[0], 308):
        iota(v("cod", lo, lo + 308), [[0, 308]], 0)
    affine(v("cl", 24, 34), v("cl", 0, 10), 1.0, 0.5)
    late[0] = False
    iota(v("sr"), [[1, P]], -192)
    iota(v("sa"), [[1, 16], [16, 24]], -192)
    mv("z_sr", v("sr", p=k1), v("sa", p=k1))
    one, eye = v("wu"), v("wt", 1536, 2048)
    fill(one, 1.0)
    wcol, whi, wlo = v("wt", 0, 512), v("wt", 512, 1024), v("wt", 1024, 1536)
    fill(wcol, -1.0)
    select(wcol, wcol, [[-16, 8], [0, 64]], ALU.is_ge, 0, 1)
    select(wcol, wcol, [[16, 8], [0, 64]], ALU.is_ge, 15, -1)
    select(wcol, wcol, [[0, 32], [1, 4], [-1, 4]], ALU.is_equal, 0, 0)
    select(eye, one, [[-1, 128], [0, 4]], ALU.is_equal, 0, 1)
    select(whi, eye, [[0, 32], [-1, 4], [1, 4]], ALU.is_ge, 0, 0)
    select(wlo, eye, [[0, 32], [1, 4], [-1, 4]], ALU.is_gt, 0, 0)
    quant(v("sumc"), v("sums"), v("wt"))
    for b in range(4):
        select(v("et", 512 * b, 512 * b + 512), one, [[-4, 128], [-1, 4]], ALU.is_equal, b, 4)
    quant(v("ec"), v("es"), v("et"))
    act(v("d0"), v("ones"), ACT.Identity, bias=cf(2), scale=0.0)

    quant(v("uc"), v("us"), v("ut"))
    op("V", lambda g, T: g.vector.tensor_copy(ap(T, v("u2c")).bitcast(dt.uint32), ap(T, v("uc")).bitcast(dt.uint32).indirect(ap(T, o_u))),
       [v("u2c")], [v("uc"), o_u], ("gather", 256))
    act(v("u2s"), ind(v("us"), o_u), ACT.Copy)

    for b in range(4):
        ts(v("stu", 32 * b, 32 * b + 24), v("ptl"), 4.0, float(b), ALU.mult, ALU.add)
    for b in range(4):
        gather("VS"[b % 2], v("x0", b, 4 * P, 4), ind(v("mm"), v("stu", 32 * b, 32 * b + 24)))
    early[0] = 1.0e6
    tt(v("kq"), v("ptl"), c_pf, ALU.add)
    for k in range(16):
        mv("s_r", v("kr", p=(k, 128, 16)), v("kq"), q="YS"[k % 2])
    early[0] = 0.0
    dma("Y", "ld_wc", u8(v("wq")), lambda T: T.wc[:], [v("wq")], [v("x0", 0, 2)], 3500)
    dma("Y", "ld_ws", lambda T: ap(T, v("wp")), lambda T: T.ws[:], [v("wp")], [v("x0", 0, 2)], 3000)
    dma("Y", "ld_v", lambda T: ap(T, v("vt")), lambda T: T.v[:], [v("vt")], [v("x0", 0, 2)], 3000)
    quant(v("vc"), v("vs"), v("vt"))

    def classes():
        for t in range(24):
            act(v("jq", P * (t % NROT), P * (t % NROT) + P), v("kr"), ACT.Sign, bias=v("kq", t, t + 1), scale=-1.0,
                acc=v("st", 216 + t, 217 + t))
        act(v("kn"), ind(v("kr"), o_pi), ACT.Copy)
        mv("s_j", v("kn", p=k1), v("page", CP, CP + P, p=k1))
        q_u = v("lu0", 384, 408)
        ts(q_u, v("st", 216, 240), 0.5, 191.5, ALU.mult, ALU.add)
        ts(v("se", 24, 48), v("ptl"), float(CP), None, ALU.add)
        copy(ind(v("ks", 0, P), q_u), v("kn"))
        act(v("tr"), ind(v("ks", 0, P), o_q), ACT.Copy)
        mv("s_g", v("se", 0, 24), v("tr", p=k1))
        copy(v("lv", 0, 24), v("se", 0, 24))
        mv("s_k", v("kl", 0, 24), v("ks", 0, P, p=k0))
        mv("s_k", v("kl", 24, 48), v("ks", 1, P + 1, p=k0))
        ts(v("sti", 0, 48), v("kl"), -0.5 + 1.0 / 1024, None, ALU.add)
        tt(v("sb", 0, 24), v("sti", 0, 24), v("sti", 24, 48), ALU.is_equal)
        copy(v("lv", 104, 128), v("sb", 0, 24))
        act(v("pn"), ind(v("page", CP, CP + 8), v("lv", 104, 128)), ACT.Copy)
        act(v("keep", 1, P + 1), ind(v("pn"), o_q), ACT.Copy)
        ts(v("sti", 48, 72), v("sti", 0, 24), 15, None, ALU.bitwise_and)
        ts(v("sti", 72, 96), v("sti", 0, 24), 4, None, ALU.logical_shift_right)
        ts(v("st", 240, 264), v("sti", 48, 72), 28.0, None, ALU.mult)
        tt(v("st", 264, 288), v("st", 240, 264), v("sti", 72, 96), ALU.add)
        tt(v("st", 288, 312), v("sb", 0, 24), c_p448, ALU.mult)
        tt(v("st", 240, 264), v("st", 264, 288), v("st", 288, 312), ALU.max)
        copy(q_u, v("st", 240, 264))
        copy(ind(v("tg"), q_u), v("pir"))
        mv("s_t", v("tag", 0, 28), v("tg", 0, M, p=k0))
        copy(v("lu0", 384, 412), v("tag", 0, 28))

    def rank(r, o, out):
        lf = "lf%d" % r
        dx, dl, hx, fl, fc, fs = ["%s%d" % (n, o) for n in ("dx", "dl", "hx", "fl", "fc", "fs")]
        row, g0 = v("pa", 512 * o, 512 * o + P), 48 * o
        tt(v(dx, L, L + P), row, v("md"), ALU.min)
        act(v(dl), v(dx, P, L + P), ACT.Abs, bias=-TINY, scale=STEP)
        tt(v(dx, 0, L), v("pa", 512 * o + L, 512 * o + P), v(dl), ALU.subtract)
        scan(v(hx), v("r0"), v(dx), 0.0, ALU.min, ALU.max)
        tt(v("gc", g0 + 24, g0 + 36), v(hx, P + 15, L + P, 16), v(hx, L + 15, P, 16), ALU.is_gt)
        act(v("gc", g0, g0 + 12), v("gc", g0 + 24, g0 + 36), ACT.Identity, bias=cf(9))
        act(v("gc", g0 + 12, g0 + 24), v("gc", g0 + 24, g0 + 36), ACT.Identity, bias=cf(10), scale=-1.0)

        def at(m):
            return LEAD + PITCH * (NF - 1 - m)
        views = [(at(m), 0) for m in range(NF)] + [(at(m) + 4 * m + d, k) for m in range(NF + 1) for k, d in ((1, 0), (2, 4), (3, 0))]
        views.sort()
        kinds = [[e for e in views if e[1] // 3 == k] for k in range(2)]
        bank = [("pa", 1024), ("pa", 1536)] if o == 0 else [("pb", 1024), ("pb", 1536)]
        m, done = NF, LEAD
        for n in CHUNKS:
            for m in range(m - 1, m - 1 - n, -1):
                tt(v(fl, 4 * at(m), 4 * at(m) + P), row, v(hx, L - 16 * m, L + P - 16 * m), ALU.is_gt)
            lo, hi = done, max(done + PITCH * n, done + 128)
            if r == 0:
                lo, hi = (0 if lo == LEAD else lo), (WORDS if m == 0 else hi)
            quant(v(fc, lo, hi), v(fs, lo, hi), v(fl, 4 * lo, 4 * hi))
            done += PITCH * n
            while views and (m == 0 or views[0][0] + 128 <= done):
                a, k = e = views.pop(0)
                y = k // 3
                mx(v(bank[y][0], bank[y][1], bank[y][1] + 128), v("sumc", 128 * k, 128 * k + 128), v("sums", 128 * k, 128 * k + 128),
                   v(fc, a, a + 128), v(fs, a, a + 128), e == kinds[y][0], e == kinds[y][-1], (r, o, y))
        scan(v("sy", 208, 308), v("c4", 3, 103), v(bank[1][0], bank[1][1], bank[1][1] + 100), 0.0, ALU.mult, ALU.add)
        tt(v("sy", 312, 408), v("sy", 211, 307), v(bank[0][0], bank[0][1], bank[0][1] + 96), ALU.add)
        scan(v("sy", 416, 512), v("dy"), v("sy", 312, 408), 0.0, ALU.add, ALU.max)
        tt(v(lf, out, out + 24), v("sy", 419, 512, 4), v("gc", g0, g0 + 24), ALU.add)

    def to_list(row, n, tb):
        tr(v(tb, 0, n), v(row, 16, 16 + n))
        tr(v(tb, n, 2 * n + 32), v(row, 0, n + 32))

    for r in range(R):
        x, xn, lu, lf, w = "x%d" % r, "x%d" % (r + 1), "lu%d" % r, "lf%d" % r, "w%d" % r

        def f(i, n=24, lf=lf):
            return v(lf, 192 + 24 * i, 192 + 24 * i + n)
        ro, ra = f(0), f(1)
        bc, bs, lc, ls = v("bc%d" % r), v("bs%d" % r), v("lc%d" % r), v("ls%d" % r)
        quant(bc, bs, v(x, 0, 4 * P))
        for i in range(2):
            c = 128 * i
            mx(v("pa", 512 * i, 512 * i + P), v("u2c", c, c + 128), v("u2s", c, c + 128), bc, bs)
        op("G", ("send", r, 0), [lc], [bc], ("send", 1), sem="arr%d" % r, inc=8, lat=1.6 * SEND)
        op("G", ("send", r, 1), [ls], [bs], ("send", 1), sem="arr%d" % r, inc=8, lat=1.6 * SEND)
        for b in range(4):
            at = 512 * (b % 2)
            mx(v("pb", at, at + P), v("ec", 128 * b, 128 * b + 128), v("es", 128 * b, 128 * b + 128), lc, ls)
            act(v("df", P * b, P * b + P), v("pb", at, at + P), ACT.Copy)
        rank(r, 0, 192)
        ts(v(lu, 0, 24), ro, 192.0, None, ALU.add)
        copy(ind(v("roo", 16, 400), v(lu, 0, 24)), v("j4"))
        to_list("roo", K, "tto")
        ts(v(lu, 48, 64), ind(v("tto"), o_b), 0.25, 240.0, ALU.mult, ALU.add)
        won = v("ll", 16 * r, 16 * r + 6)
        op("G", ("send", r, 2), [won], [v(lu, 48, 54)], ("send", 1), sem="arl%d" % r, inc=8, lat=SEND)
        for b in range(4):
            gather(GD[r][b], v(x, 4 * P + b, 4 * (P + K), 4), ind(v("df", P * b, P * b + P), won))
        h, u_, km, k2 = f(2), f(3), f(5), f(4)
        s4 = v("s4%d" % r, 0, 24)
        act(f(6), ro, ACT.Sign, bias=-95.5)
        affine(h, f(6), -48.0, -48.0)
        act(u_, ro, ACT.Relu, bias=-FAR, scale=-2 * FAR)
        tt(k2, ro, u_, ALU.subtract)
        tt(km, k2, h, ALU.add)
        affine(f(7), km, 4.0, 4.0 * P - 960.0)
        tt(s4, f(7), c_j4, ALU.max)
        mv("r_s%d" % r, v("sr", p=k0), s4, 1.5 * MOVE)
        act(v("nr"), ind(v("sr"), o_pi), ACT.Copy)
        rank(r, 1, 216)
        ts(v(lu, 24, 48), ra, 192.0, None, ALU.add)
        copy(ind(v("roa", 16, 400), v(lu, 24, 48)), v("nr"))
        to_list("roa", A, "tta")
        tt(v(lf, 576, 672), ind(v("tta"), o_z), v("cz"), ALU.add)
        copy(v(lu, 112, 208), v(lf, 576, 672))
        for b in range(4):
            gather(GZ[r][b], v("zt", b, 4 * A, 4), ind(v(x, 0, 4 * (P + K)), v(lu, 112 + 16 * b, 122 + 16 * b)))
        quant(v("zc"), v("zs"), v("zt"))
        act(f(8), ra, ACT.Relu, bias=2 * FAR * (192.5 - A), scale=2 * FAR)
        affine(f(15), ra, 4.0, 4.0 * (P + K + 192) - 960.0)
        tt(f(9), f(15), f(8), ALU.subtract)
        tt(f(10), f(9), s4, ALU.max)
        for b in range(4):
            affine(v(lf, 24 * b, 24 * b + 24), f(10), 1.0, 960.0 + b)
        copy(v(lu, 208, 304), v(lf, 0, 96))
        for b in range(4):
            mx(v("pb", 512 * b, 512 * b + A), v("wq", 128 * b, 128 * b + 128), v("wp", 128 * b, 128 * b + 128), v("zc"), v("zs"))
            act(v("rb", b, 4 * A, 4), v("pb", 512 * b, 512 * b + A), ACT.Relu, scale=0.03125)
            if b % HS[r] == HS[r] - 1:
                for e in range(b + 1 - HS[r], b + 1) if HS[r] < 4 else [0]:
                    st = 4 if HS[r] < 4 else 1
                    tt(v(x, 4 * (P + K) + e, 2560, st), v("rb", e, 4 * A, st), v("zt", e, 4 * A, st), ALU.add)
        nc = 1 if r + 1 < R else 3
        for c in range(nc):
            for b in range(4):
                lo, n = 208 + 24 * b + 8 * c, 24 // nc
                gather(GF[r][b], v(xn, 512 * c + b, 512 * c + 64 * n, 4), ind(v(x), v(lu, lo, lo + n)))

        if r == 0:
            classes()
        affine(f(14), km, 1.0, float(ZS[r] + L))
        tt(v("se", 24, 48), v("se", 24, 48), f(14), ALU.max)
        copy(v(lu, 360, 384), v("se", 24, 48))
        kind = v("cr", 0, P)
        act(kind, ind(v("cod"), v(lu, 360, 384)), ACT.Copy)
        act(v(w, ZQ, ZQ + P), ind(kind, v("lv", 0, 24)), ACT.Relu, bias=1.0, scale=-1.0)
        scan(v(w, AO, AO + P), v("keep", 0, P), v(w, ZQ, ZQ + P), 0.0, ALU.mult, ALU.add)
        for s in range(r):
            act(v(w, ZS[s], ZS[s] + L), ind(kind, v("lv", 44 + 24 * s, 56 + 24 * s)), ACT.Relu, bias=2.0 + 2 * s, scale=-1.0)
            tt(v(w, ZS[s] + L, ZS[s] + L + K), v(w, ZS[s] + K, ZS[s] + L), v(w, ZS[s], ZS[s] + K), ALU.add)
            act(v("pz", A, 2 * A), ind(kind, v("lu%d" % s, 176, 186)), ACT.Relu, bias=3.0 + 2 * s, scale=-1.0)
            act(v(w, ZS[s] + L + K, ZS[s] + L + K + A), ind(v("pz", A, 2 * A + 16), v("lv", 80 + 16 * s, 90 + 16 * s)), ACT.Copy)
        act(v(w, CP, CP + M), ind(v(w, AO, ZS[r]), v(lu, 384, 412)), ACT.Copy)
        act(v("mr"), ind(v(w), v(lu, 360, 384)), ACT.Sign, bias=-1.5)
        act(v("mk"), ind(v("mr"), v(lu, 176, 186)), ACT.Relu)
        scan(v("pk", 0, A), v("d0", 0, A), v("mk"), 0.0, ALU.mult, ALU.add)
        if r + 1 < R:
            act(v("pn"), ind(v("pk"), v(lu, 24, 48)), ACT.Copy)
            act(v("rj%d" % r), ind(v("pn"), o_q), ACT.Copy)
            act(v("cr", P, 2 * P), ind(v("roo", 16, 400), o_q), ACT.Copy)
            mv("r_l%d" % r, v("pj%d" % r, 112, 136), v("cr", P, 2 * P, p=k0))
            affine(f(13), v("pj%d" % r, 112, 136), 0.25, 240.0)
            copy(v("lv", 32 + 24 * r, 56 + 24 * r), f(13))
            scan(v("pz", 0, A), v("ones", 0, A), v("mk"), 0.0, ALU.mult, ALU.add)
            for t in range(10):
                act(v("jq", P * (t % NROT), P * (t % NROT) + A), v("pz", 0, A), ACT.Sign, bias=v("cl", 24 + t, 25 + t), scale=-1.0,
                    acc=v("st", t, t + 1))
            ts(v("lv", 80 + 16 * r, 90 + 16 * r), v("st", 0, 10), 0.5, A / 2, ALU.mult, ALU.add)
        else:
            copy(ind(v("rj%d" % r), v(lu, 192, 202)), v("pk", 0, A))
        pj = "pj%d" % r
        mv("r_p%d" % r, v(pj, 0, 24), v("rj%d" % r, p=k0))
        mv("r_p%d" % r, v(pj, 24, 48), v("rj%d" % r, p=k1))
        act(v("fre"), v(w, CP, CP + M), ACT.Relu, bias=1.0, scale=-1.0)
        scan(v("pf"), v("d0"), v("fre"), -224.0, ALU.mult, ALU.add)
        act(v("pp"), ind(v("pf"), o_t), ACT.Copy)
        mv("r_f%d" % r, v(pj, 48, 76), v("pp", p=k0))
        mv("r_f%d" % r, v(pj, 80, 108), v("pp", p=k1))
        pl = 768
        affine(v(lf, 736, 764), v(pj, 80, 108), FAR, float(223 + ZS[r] + L - AO) - FAR)
        tt(v(lf, pl, pl + 28), v(pj, 48, 76), v(lf, 736, 764), ALU.add)
        tt(v("tag", 0, 28), v("tag", 0, 28), v(lf, pl, pl + 28), ALU.max)
        nu = "lu%d" % (r + 1) if r + 1 < R else "stu"
        n0 = 384 if r + 1 < R else 0
        copy(v(nu, n0, n0 + 28), v("tag", 0, 28))
        affine(f(12), v(pj, 24, 48), FAR, float(ZS[r] + L + K - 1) - FAR)
        tt(f(11), f(12), v(pj, 0, 24), ALU.add)
        tt(v("se", 24, 48), v("se", 24, 48), f(11), ALU.max)

    copy(ind(v("page", AO, END), v("stu", 0, 28)), v("page", CP, CP + M))
    copy(v("stu", 32, 56), v("se", 24, 48))
    act(v("tr"), ind(v("page"), v("stu", 32, 56)), ACT.Copy)
    dma("S", "o_m", lambda T: T.om[:], lambda T: ap(T, v("tr", p=k0)), [], [v("tr")], 2200)
    for c in range(3):
        lo, hi = 128 * c, 128 * c + 128
        quant(v("qc", lo, hi), v("qs", lo, hi), v("x3", 4 * lo, 4 * hi))
        mx(v("pa", 512 * c, 512 * c + 128), v("vc"), v("vs"), v("qc", lo, hi), v("qs", lo, hi))
        dma("Y", "o_c", lambda T, lo=lo, hi=hi: T.oc[:, 4 * lo:4 * hi], u8(v("qc", lo, hi)), [], [v("qc", lo, hi)], 2500)
        gather("SSV"[c], v("yb", lo, hi), v("pa", 512 * c, 512 * c + 128))
        dma("Y", "o_y", lambda T, lo=lo, hi=hi: T.y[:, lo:hi], lambda T, lo=lo, hi=hi: ap(T, v("yb", lo, hi)), [], [v("yb", lo, hi)], 2500)
    for k in range(4):
        dma("S", "o_s", lambda T, k=k: T.osc[4 * k:4 * k + 4, :], lambda T, k=k: T.qs[32 * k:32 * k + 4, :], [], [v("qs")], 2200)
    return ops


def region(x):
    name, lo, hi, step, p = x
    if SCRATCH[name][0] == "psum":
        lo, hi, step = lo // 512 * 512, (hi + 511) // 512 * 512, 1
    if step == 1:
        cm = ((1 << (hi - lo)) - 1) << lo
    else:
        cm = sum(1 << c for c in range(lo, hi, step))
    pm = (1 << 128) - 1 if p is None else sum(1 << q for q in range(p[0], p[1], p[2]))
    return name, cm, pm


def plan():
    ops = build()
    n = len(ops)
    hist = {}
    groups = {}
    for i, o in enumerate(ops):
        if o["sem"]:
            groups.setdefault(o["sem"], []).append(i)
    for i, o in enumerate(ops):
        dep = set()
        acc = [(region(x), False) for x in o["r"]] + [(region(x), True) for x in o["w"]]
        for (name, cm, pm), wr in acc:
            psum = SCRATCH[name][0] == "psum"
            for j, cj, pj, wj in hist.get(name, []):
                if j != i and cj & cm and pj & pm and (wr or wj or (psum and ops[j]["eng"] != o["eng"])):
                    dep.add(j)
        for (name, cm, pm), wr in acc:
            h = hist.setdefault(name, [])
            if wr:
                h[:] = [e for e in h if e[1] & ~cm or e[2] & ~pm]
            h.append((i, cm, pm, wr))
        for j in list(dep):
            if ops[j]["sem"]:
                dep.update(groups[ops[j]["sem"]])
        dep.discard(i)
        o["dep"] = sorted(dep)
        o["ix"] = i
    first = [o for o in ops if o["sem"] == "arl0"][0]["dep"]
    for o in ops:
        if o["late"]:
            o["dep"] = sorted(set(o["dep"] + first))
    succ = [[] for _ in range(n)]
    for i, o in enumerate(ops):
        for j in o["dep"]:
            succ[j].append(i)
    figures = []
    for fix, least, wake, scatter, gather, product, slow, issue in CASES:
        cost = []
        for o in ops:
            k, m = o["cost"]
            extra = 18.0 if o["eng"] == "S" else 0.0
            cost.append({"plain": extra + fix + max(least, m), "gather": extra + 60 + gather * m, "scatter": 60 + scatter * m,
                         "product": 30 + product * m, "fixed": m, "send": issue}[k])
        figures.append((cost, [o["lat"] * slow for o in ops], wake))

    def replay(order, case):
        cost, lat, wake = figures[case]
        free, end = {e: 0.0 for e in "VSPGY"}, [0.0] * n
        for i in order:
            o = ops[i]
            t = free[o["eng"]]
            for j in o["dep"]:
                t = max(t, end[j] + (0.0 if o["grp"] and o["grp"] == ops[j]["grp"] else wake))
            free[o["eng"]] = t + cost[i]
            end[i] = t + cost[i] + lat[i]
        return max(end)

    def schedule(prio, before, after, back, case):
        cost, lat, wake = figures[case]
        left = [len(x) for x in before]
        ready_at = [lat[i] if back else 0.0 for i in range(n)]
        ready = {e: [] for e in "VSPGY"}
        for i in range(n):
            if left[i] == 0:
                ready[ops[i]["eng"]].append(i)
        free = {e: 0.0 for e in ready}
        order, start, end = [], [0.0] * n, [0.0] * n
        while len(order) < n:
            best = None
            for e, lst in ready.items():
                if lst:
                    t = max(free[e], min(ready_at[i] for i in lst))
                    if best is None or t < best[0]:
                        best = (t, e)
            t, e = best
            top = max(ready[e], key=lambda i: prio[i])
            i = max([i for i in ready[e] if ready_at[i] <= t], key=lambda i: prio[i])
            if ready_at[top] > t and ready_at[top] - t < LOOK[0] * cost[i] and prio[top] > prio[i] + LOOK[1]:
                i, t = top, ready_at[top]
            ready[e].remove(i)
            start[i] = t
            free[e] = t + cost[i]
            end[i] = free[e] + (0.0 if back else lat[i])
            order.append(i)
            for s in after[i]:
                gap = 0.0 if ops[i]["grp"] and ops[i]["grp"] == ops[s]["grp"] else wake
                ready_at[s] = max(ready_at[s], end[i] + gap + (lat[s] if back else 0.0))
                left[s] -= 1
                if left[s] == 0:
                    ready[ops[s]["eng"]].append(s)
        return order, start, end

    pred = [o["dep"] for o in ops]
    kept, x = None, SEED[0]
    for case in range(len(CASES)):
        cost, lat, wake = figures[case]
        prio = [0.0] * n
        for i in range(n - 1, -1, -1):
            prio[i] = cost[i] + lat[i] + ops[i]["early"] + max([prio[s] + wake for s in succ[i]] + [0.0])
        local = None
        for turn in range(TURNS[0]):
            order, start, end = schedule(prio, pred, succ, False, case)
            times = [replay(order, c) for c in range(WEIGHED)]
            if kept is None or sum(times) < kept[0]:
                kept = (sum(times), order, start, end, times, case)
            if local is None or sum(times) < local:
                local = sum(times)
                prio = base = schedule(end, succ, pred, True, case)[2]
            else:
                prio = []
                for i in range(n):
                    x = (x * 1103515245 + 12345) % 2147483648
                    prio.append(base[i] + SEED[1] * (x / 2147483648.0))
                if turn % 2:
                    prio = schedule(schedule(prio, pred, succ, False, case)[2], succ, pred, True, case)[2]
    order = kept[1]
    for i in order:
        ops[i]["start"], ops[i]["done"], ops[i]["cost"] = kept[2][i], kept[3][i], figures[kept[5]][0][i]
    ops[order[0]]["times"] = kept[4]
    count = {}
    for i in order:
        o = ops[i]
        s = o["sem"] or "q" + o["eng"]
        count[s] = count.get(s, 0) + o["inc"]
        o["at"] = (s, count[s])
    seen = {e: {} for e in "VSPGY"}
    for i in order:
        o = ops[i]
        need = {}
        for j in o["dep"]:
            if o["grp"] and o["grp"] == ops[j]["grp"]:
                continue
            s, c = ops[j]["at"]
            need[s] = max(need.get(s, 0), c)
        o["waits"] = []
        for s, c in sorted(need.items()):
            if seen[o["eng"]].get(s, 0) < c:
                seen[o["eng"]][s] = c
                o["waits"].append((s, c))
    return [ops[i] for i in order], count


PLAN, COUNT = plan()
SEMAPHORES = sorted(COUNT) + ["snt"]


def rank_program(g, core, T, topo):
    rank = T.rank_of(core)
    if rank is None:
        return
    nxt = T.cores[(rank + 1) % len(T.cores)]
    rid, pid = topo.addr(nxt)[:2]
    eng = topo.engines(core, nxt)
    mask = sum(1 << e for e in eng[:8])
    queue = {"V": g.vector, "S": g.scalar, "P": g.tensor, "G": g, "Y": g.sync}
    for o in PLAN:
        q = queue[o["eng"]]
        for s, c in o["waits"]:
            q.wait_ge(T.sem[s], c)
        if isinstance(o["fn"], tuple):
            src, dst = ap(T, o["r"][0]), ap(T, o["w"][0])
            if o["fn"][2] == 0:
                src, dst = src.bitcast(dt.uint8), dst.bitcast(dt.uint8)
            g.remote_dma(dst, src, T.sem[o["sem"]], T.sem["snt"], pid, rid, mask)
        else:
            o["fn"](g, T).then_inc(T.sem[o["at"][0]], o["inc"])
    for s in sorted(COUNT):
        g.wait_ge(T.sem[s], COUNT[s])
    g.wait_ge(T.sem["snt"], 24 * R)
